import numpy as np, ml_dtypes
CORES = [2,6,10,14,18,22,26,30]
N = 8
import mx_ref
BF = ml_dtypes.bfloat16
def entries(a):
    return np.ascontiguousarray(a.T).reshape(-1)
def table(e):
    return np.ascontiguousarray(np.reshape(e, (-1, 16)).T).astype(np.int32)
def tile(rs):
    return np.stack(rs, axis=2).reshape(128, -1).astype(BF)
def cut(t, i, w=512):
    return t[:, w * i:w * i + w]
def f(rng, *shape):
    return mx_ref.flush((rng.standard_normal(shape, dtype=np.float32) * np.exp2(rng.integers(-2, 3, shape[:-1] + (1,)))).astype(BF))
def wide(rng, *shape, cols=0):
    v = rng.standard_normal(shape, dtype=np.float32) * np.exp2(rng.integers(-12, 13, shape)).astype(np.float32)
    if cols: v *= np.repeat(np.exp2(rng.integers(-cols, cols + 1, shape[:-2] + (1, shape[-1] // 4))) * (rng.random(shape[:-2] + (1, shape[-1] // 4)) > 0.0625), 4, axis=-1).astype(np.float32)
    return mx_ref.flush(v.astype(BF))
T, CAPP, P = 512, 48, 256
SL = N * CAPP
G = 1
def pieces(rng, how):
    if how == "ones": n = np.ones((G, SL), int)
    elif how == "full":
        n = T - rng.integers(0, 8, (G, SL)); n[:, ::4] = T
    elif how == "powers":
        k = [1 << i for i in range(T.bit_length())]; k = sorted(set(k + [i + 1 for i in k if i < T]))
        n = rng.permuted(np.tile(np.resize(k, SL), (G, 1)), axis=1)
    else: n = np.where(rng.random((G, SL)) < 0.5, rng.integers(1, T + 1, (G, SL)), np.clip(np.exp2(rng.uniform(0, T.bit_length() - 1, (G, SL))).astype(int), 1, T))
    s = rng.integers(0, T - n + 1)
    if how == "full": s[:] = 0
    if how == "nested":
        for g in range(G):
            for r in range(N):
                m = rng.integers(0, T)
                b = np.sort(rng.choice(rng.integers(0, m + 1, 16), CAPP)); e = np.sort(rng.choice(rng.integers(m, T, 16), CAPP))[::-1]
                k = r * CAPP + rng.permutation(CAPP); s[g, k] = b; n[g, k] = e - b + 1
    return s, n
def lists(rng, how="any", every=False):
    held = np.zeros((N, N, CAPP), bool)
    for r in range(N):
        n = rng.integers(0, CAPP + 1, N); n[(r + rng.integers(1, N)) % N] = CAPP
        for q in range(N): held[q, r, rng.permutation(CAPP)[:CAPP if every else n[q]]] = True
    d = {"lo": [], "ln": [], "pf": [], "pg": []}
    for q in range(N):
        s, n = pieces(rng, how); e = ~held[q].reshape(-1)
        s[:, e] = -1; n[:, e] = 0
        d["lo"].append(table(s)); d["ln"].append(table(n))
    who = rng.permutation(N)
    for r in range(N):
        k = rng.permutation(np.flatnonzero(held[:, r]))
        first = rng.permutation(np.resize(k, P))
        second = np.where(rng.random(P) < 0.25, -1, rng.choice(k, P))
        if how == "ones":
            if r == who[0]:
                first[rng.permutation(P)[:P // 2]] = k[0]; second[rng.permutation(P)[:P // 2]] = k[0]
            if r == who[1]: second[:] = -1
            if r == who[2]: second = rng.choice(k, P)
        d["pf"].append(table(first))
        d["pg"].append(table(second))
    return {k: np.stack(t) for k, t in d.items()}
def setup_inputs(rng):
    return {"x": f(rng, N, 128, 4 * T), "a": f(rng, N, 128, 2048), "u": f(rng, N, 128, 512), "v": f(rng, N, 128, 512), **lists(rng)}
def setup_inputs_ones(rng):
    return {**setup_inputs(rng), **lists(rng, "ones")}
def setup_inputs_full(rng):
    return {**setup_inputs(rng), **lists(rng, "full", True)}
def setup_inputs_powers(rng):
    return {**setup_inputs(rng), **lists(rng, "powers", True)}
def setup_inputs_nested(rng):
    return {**setup_inputs(rng), **lists(rng, "nested", True)}
def setup_inputs_spread(rng):
    d = setup_inputs(rng); d["x"] = wide(rng, N, 128, 4 * T, cols=8); return d
def check_inputs(d):
    b = []; held = []
    for q in range(N):
        s, n = entries(d["lo"][q]).reshape(G, -1), entries(d["ln"][q]).reshape(G, -1)
        e = s == -1; held.append(~e[0])
        if s.min() < -1 or s.max() >= T or (e != e[:1]).any(): b.append("lo")
        if (n[e] != 0).any() or (n[~e] < 1).any() or (n[~e] > T - s[~e]).any(): b.append("ln")
    for r in range(N):
        h = np.concatenate([held[q][r * CAPP:r * CAPP + CAPP] for q in range(N)])
        for k, least in (("pf", 0), ("pg", -1)):
            j = entries(d[k][r])
            if j.min() < least or j.max() >= SL or not h[j[(j >= 0) & (j < SL)]].all(): b.append(k)
    return b
def reference(x, a, u, v, lo, ln, pf, pg):
    sent = []
    for q in range(N):
        X = mx_ref.quantize(x[q])
        Z = np.stack([mx_ref.matmul(mx_ref.quantize(np.ascontiguousarray(cut(a[q], i))), X) for i in range(4)])
        h = np.maximum(Z, np.float32(0)) * np.float32(0.05)
        s, n = entries(lo[q]), entries(ln[q])
        R = np.zeros((4, 128, SL), np.float32)
        for k in range(SL):
            if n[k]: R[:, :, k] = h[:, :, s[k]:s[k] + n[k]].max(axis=2)
        sent.append([mx_ref.quantize(np.ascontiguousarray(tile([R[i][:, CAPP * r:CAPP * r + CAPP] for i in range(4)]))) for r in range(N)])
    y = np.zeros((N, 128, P), np.float32)
    for r in range(N):
        V, U = mx_ref.quantize(v[r]), mx_ref.quantize(u[r])
        zv = np.concatenate([mx_ref.matmul(V, sent[q][r]) for q in range(N)], axis=1)
        zu = np.concatenate([mx_ref.matmul(U, sent[q][r]) for q in range(N)], axis=1)
        first, second = entries(pf[r]), entries(pg[r])
        y[r] = zv[:, first]
        two = second >= 0
        y[r][:, two] += zu[:, second[two]]
    return {"y": y}

@@ -1,0 +1,403 @@
+from concourse.bass import DstId, RemoteDMATransfer
+from concourse.mybir import dt, AluOpType, ActivationFunctionType
+
+N, CAPP, NT, P = 8, 48, 512, 256
+SL = N * CAPP
+LC = SL // 16
+NB = NT // 4
+LEV = NB.bit_length() - 2
+O_H, O_S4, O_P4 = 0, NT, 2 * NT
+BD = 3 * NT + LEV * NB
+W = BD + (LEV + 1) * NB
+HALF = SL // 2
+M_LEV = NT
+M_TRI = M_LEV + LEV * NB
+M_ALL = M_TRI + 3 * SL
+ZCOL = SL
+
+SCRATCH = {
+    "xs": ("sbuf", [128, 4 * NT], "bfloat16"),
+    "as_": ("sbuf", [128, 2048], "bfloat16"),
+    "us": ("sbuf", [128, 512], "bfloat16"),
+    "vs": ("sbuf", [128, 512], "bfloat16"),
+    "xq": ("sbuf", [128, NT], "float8_e4m3fn_x4"),
+    "xp": ("sbuf", [128, NT], "uint8"),
+    "aq": ("sbuf", [128, 512], "float8_e4m3fn_x4"),
+    "ap_": ("sbuf", [128, 512], "uint8"),
+    "uq": ("sbuf", [128, 128], "float8_e4m3fn_x4"),
+    "up": ("sbuf", [128, 128], "uint8"),
+    "vq": ("sbuf", [128, 128], "float8_e4m3fn_x4"),
+    "vp": ("sbuf", [128, 128], "uint8"),
+    "z": ("psum", [128, 4096], "float32"),
+    "win": ("sbuf", [128, 4 * W], "bfloat16"),
+    "mk": ("sbuf", [128, M_ALL], "bfloat16"),
+    "tile": ("sbuf", [128, 4 * SL], "bfloat16"),
+    "fq": ("sbuf", [128, HALF], "float8_e4m3fn_x4"),
+    "fp": ("sbuf", [128, HALF], "uint8"),
+    "nq": ("sbuf", [128, HALF], "float8_e4m3fn_x4"),
+    "np_": ("sbuf", [128, HALF], "uint8"),
+    "rfq": ("sbuf", [128, HALF], "float8_e4m3fn_x4"),
+    "rfp": ("sbuf", [128, HALF], "uint8"),
+    "rnq": ("sbuf", [128, HALF], "float8_e4m3fn_x4"),
+    "rnp": ("sbuf", [128, HALF], "uint8"),
+    "zv": ("sbuf", [128, SL], "float32"),
+    "zu": ("sbuf", [128, SL + 16], "float32"),
+    "gy": ("sbuf", [128, P], "float32"),
+    "ys": ("sbuf", [128, P], "float32"),
+    "offs": ("sbuf", [128, 4 * LC], "uint16"),
+    "offl": ("sbuf", [128, 4 * LC], "uint16"),
+    "los": ("sbuf", [128, LC], "int32"),
+    "lns": ("sbuf", [128, LC], "int32"),
+    "l_t": ("sbuf", [128, LC], "int32"),
+    "l_lr": ("sbuf", [128, 2 * LC], "int32"),
+    "l_q": ("sbuf", [128, 2 * LC], "int32"),
+    "l_12": ("sbuf", [128, 2 * LC], "int32"),
+    "l_ab": ("sbuf", [128, 2 * LC], "int32"),
+    "l_ad": ("sbuf", [128, 2 * LC], "int32"),
+    "l_cr": ("sbuf", [128, LC], "int32"),
+    "l_c12": ("sbuf", [128, 2 * LC], "int32"),
+    "l_mm": ("sbuf", [128, 2 * LC], "int32"),
+    "l_mid": ("sbuf", [128, 2 * LC], "int32"),
+    "l_sa": ("sbuf", [128, LEV * LC], "int32"),
+    "l_sb": ("sbuf", [128, LEV * LC], "int32"),
+    "l_ne": ("sbuf", [128, LEV * LC], "int32"),
+    "l_am": ("sbuf", [128, 2 * LC], "int32"),
+    "l_amm": ("sbuf", [128, 2 * LC], "int32"),
+    "l_amp": ("sbuf", [128, 2 * LC], "int32"),
+    "l_w": ("sbuf", [128, 2 * LC], "int32"),
+    "l_e": ("sbuf", [128, 3 * LC], "int32"),
+    "l_f": ("sbuf", [128, LC], "int32"),
+    "l_k": ("sbuf", [128, LC], "int32"),
+    "l_kw": ("sbuf", [128, 2 * LC], "int32"),
+    "l_o": ("sbuf", [128, 4 * LC], "int32"),
+    "pfs": ("sbuf", [128, P // 16], "int32"),
+    "pgs": ("sbuf", [128, P // 16], "int32"),
+    "pgt": ("sbuf", [128, P // 16], "int32"),
+    "pgn": ("sbuf", [128, P // 16], "int32"),
+    "pfo": ("sbuf", [128, P // 16], "uint16"),
+    "pgo": ("sbuf", [128, P // 16], "uint16"),
+}
+for _i in range(4):
+    SCRATCH["g%d" % _i] = ("sbuf", [128, 3 * SL], "bfloat16")
+    SCRATCH["m%d" % _i] = ("sbuf", [128, 3 * SL], "bfloat16")
+
+SEMAPHORES = (["lst", "lx", "la0", "la1", "la2", "luv", "lpl", "rep", "vm", "vc", "qx", "qa0", "qa1", "qa2", "quv",
+               "qf", "qn", "zero", "pl", "own", "arrf", "arrn", "loc", "mfv", "mfu", "mnv", "mnu", "zvs", "zus",
+               "gy0", "gy1", "y0", "y1", "yo", "tl", "tlf", "tln", "g3f", "g3n", "m3f", "m3n"]
+              + ["mm%d" % i for i in range(4)] + ["rl%d" % i for i in range(4)]
+              + ["p4_%d" % i for i in range(4)] + ["bd%d" % i for i in range(4)]
+              + ["ga%d" % i for i in range(3)] + ["me%d" % i for i in range(3)])
+
+ADD, SUB, MUL, MAX, MIN = AluOpType.add, AluOpType.subtract, AluOpType.mult, AluOpType.max, AluOpType.min
+GE, GT, LT, NEQ = AluOpType.is_ge, AluOpType.is_gt, AluOpType.is_lt, AluOpType.not_equal
+SHR = AluOpType.arith_shift_right
+RELU, COPY = ActivationFunctionType.Relu, ActivationFunctionType.Copy
+
+
+def rev(t, lo, hi, step=1):
+    return t[:, hi - 1:(lo - 1 if lo > 0 else None):-step]
+
+
+def engine_plan(core, dests, topo):
+    off = [d for d in dests if topo.chip(d) != topo.chip(core)]
+    pool = topo.engines(core, off[0])
+    per = 1
+    while 2 * per * len(off) <= len(pool):
+        per *= 2
+    masks, used = {}, []
+    for k, d in enumerate(off):
+        masks[d] = pool[k * per:(k + 1) * per]
+        used += masks[d]
+    for d in dests:
+        if d not in masks:
+            free = [e for e in topo.engines(core, d) if e not in pool]
+            masks[d] = free[:2]
+            used += masks[d]
+    return masks
+
+
+def rank_program(g, core, T, topo):
+    rank = T.rank_of(core)
+    if rank is None:
+        return
+    cores = T.cores
+    S = T.sem
+    v, s, te, sy = g.vector, g.scalar, g.tensor, g.sync
+
+    def group(c, far):
+        a = topo.chip(c)
+        return [q for q in range(N)
+                if (topo.chip(cores[q]) != a and not topo.mates(topo.chip(cores[q]), a)) == far]
+
+    far, near = group(core, True), group(core, False)
+    fs, ns = far[0] * CAPP, near[0] * CAPP
+
+    s.dma_start(T.los[0:16, :], T.lo[:, :]).then_inc(S.lst, 16)
+    sy.dma_start(T.lns[0:16, :], T.ln[:, :]).then_inc(S.lst, 16)
+    sy.dma_start(T.xs[:, :], T.x[:, :]).then_inc(S.lx, 16)
+    sy.dma_start(T.as_[:, 0:512], T.a[:, 0:512]).then_inc(S.la0, 16)
+    sy.dma_start(T.as_[:, 512:1024], T.a[:, 512:1024]).then_inc(S.la1, 16)
+    sy.dma_start(T.as_[:, 1024:2048], T.a[:, 1024:2048]).then_inc(S.la2, 16)
+
+    v.memset(T.mk[:, :], 1.0).then_inc(S.vm, 1)
+    v.memset(T.zu[:, ZCOL:ZCOL + 16], 0.0).then_inc(S.zero, 1)
+    v.wait_ge(S.vm, 1)
+    v.memset(T.mk[:, 0:NT:4], 0.0).then_inc(S.vm, 1)
+    for k in range(1, LEV + 1):
+        b = M_LEV + (k - 1) * NB
+        v.memset(T.mk[:, b:b + NB:1 << k], 0.0).then_inc(S.vm, 1)
+    v.memset(T.mk[:, M_TRI:M_ALL:3], 0.0).then_inc(S.vm, 1)
+    n_masks = LEV + 3
+
+    cnt = [0]
+
+    def done(ins):
+        ins.then_inc(S.vc, 1)
+        cnt[0] += 1
+
+    def sync_v():
+        v.wait_ge(S.vc, cnt[0])
+
+    def pa(t, a=None, b=None):
+        return t[0:16, :] if a is None else t[0:16, a:b]
+
+    L, L2 = LC, 2 * LC
+
+    def lists_one():
+        v.wait_ge(S.lst, 32)
+        done(v.tensor_tensor(pa(T.l_t), pa(T.los), pa(T.lns), ADD))
+        done(v.tensor_scalar(pa(T.l_lr, 0, L), pa(T.los), 0.0, None, MAX))
+        sync_v()
+        done(v.tensor_scalar(pa(T.l_lr, L, L2), pa(T.l_t), -1.0, 0.0, ADD, MAX))
+        sync_v()
+        done(v.tensor_scalar(pa(T.l_q), pa(T.l_lr), 2, None, SHR))
+        done(v.tensor_scalar(pa(T.l_12, 0, L), pa(T.l_lr, 0, L), 1.0, None, ADD))
+        done(v.tensor_scalar(pa(T.l_12, L, L2), pa(T.l_lr, 0, L), 2.0, None, ADD))
+        sync_v()
+        done(v.tensor_scalar(pa(T.l_ab, 0, L), pa(T.l_q, 0, L), 1.0, None, ADD))
+        done(v.tensor_scalar(pa(T.l_ab, L, L2), pa(T.l_q, L, L2), -1.0, None, ADD))
+        done(v.tensor_scalar(pa(T.l_ad, 0, L), pa(T.l_q, 0, L), float(BD + 1), None, ADD))
+        done(v.tensor_scalar(pa(T.l_ad, L, L2), pa(T.l_q, L, L2), float(BD - 1), None, ADD))
+        done(v.tensor_tensor(pa(T.l_cr), pa(T.l_q, L, L2), pa(T.l_q, 0, L), GT))
+        done(v.tensor_tensor(pa(T.l_mm, 0, L), pa(T.l_12, 0, L), pa(T.l_lr, L, L2), MIN))
+        done(v.tensor_tensor(pa(T.l_mm, L, L2), pa(T.l_12, L, L2), pa(T.l_lr, L, L2), MIN))
+        sync_v()
+        for j in range(1, LEV + 1):
+            done(v.tensor_scalar(pa(T.l_sa, (j - 1) * L, j * L), pa(T.l_ab, 0, L), j, None, SHR))
+            done(v.tensor_scalar(pa(T.l_sb, (j - 1) * L, j * L), pa(T.l_ab, L, L2), j, None, SHR))
+        done(v.tensor_tensor(pa(T.l_mid, 0, L), pa(T.l_ab, L, L2), pa(T.l_ab, 0, L), GE))
+        done(v.tensor_tensor(pa(T.l_mid, L, L2), pa(T.l_ab, L, L2), pa(T.l_ab, 0, L), GE))
+        done(v.tensor_scalar(pa(T.l_c12, 0, L), pa(T.l_cr), float(O_S4), None, MUL))
+        done(v.tensor_scalar(pa(T.l_c12, L, L2), pa(T.l_cr), float(O_P4), None, MUL))
+        done(v.tensor_tensor(pa(T.l_am), pa(T.l_ad), pa(T.l_mm), SUB))
+
+    def lists_two():
+        sync_v()
+        done(v.tensor_tensor(pa(T.l_ne), pa(T.l_sa), pa(T.l_sb), NEQ))
+        done(v.tensor_tensor(pa(T.l_amm), pa(T.l_am), pa(T.l_mid), MUL))
+        done(v.tensor_tensor(pa(T.l_o, 0, L2), pa(T.l_lr), pa(T.l_c12), ADD))
+        done(v.tensor_scalar(pa(T.l_w, 0, L), pa(T.l_mid, 0, L), float(NB), None, MUL))
+        done(v.tensor_scalar(pa(T.l_w, L, L2), pa(T.l_mid, L, L2), float(-NB), None, MUL))
+        sync_v()
+        done(v.tensor_tensor(pa(T.l_e), pa(T.l_ne, 0, 3 * L), pa(T.l_ne, 3 * L, 6 * L), ADD))
+        done(v.tensor_tensor(pa(T.l_amp), pa(T.l_amm), pa(T.l_mm), ADD))
+        sync_v()
+        done(v.tensor_tensor(pa(T.l_f), pa(T.l_e, 0, L), pa(T.l_e, L, L2), ADD))
+        sync_v()
+        done(v.tensor_tensor(pa(T.l_k), pa(T.l_f), pa(T.l_e, L2, 3 * L), ADD))
+        sync_v()
+        done(v.tensor_tensor(pa(T.l_kw, 0, L), pa(T.l_k), pa(T.l_w, 0, L), MUL))
+        done(v.tensor_tensor(pa(T.l_kw, L, L2), pa(T.l_k), pa(T.l_w, L, L2), MUL))
+        sync_v()
+        done(v.tensor_tensor(pa(T.l_o, L2, 4 * L), pa(T.l_kw), pa(T.l_amp), ADD))
+        sync_v()
+        done(v.tensor_copy(pa(T.offl), pa(T.l_o)))
+
+    lists_one()
+
+    def quant_a(lo, hi, load, q):
+        v.wait_ge(load, 16)
+        v.quantize_mx(T.aq[:, lo:hi], T.ap_[:, lo:hi], T.as_[:, 4 * lo:4 * hi]).then_inc(q, 1)
+
+    v.wait_ge(S.lx, 16)
+    v.quantize_mx(T.xq[:, :], T.xp[:, :], T.xs[:, :]).then_inc(S.qx, 1)
+    quant_a(0, 128, S.la0, S.qa0)
+    lists_two()
+    n_lists = cnt[0]
+    quant_a(128, 256, S.la1, S.qa1)
+
+    sy.wait_ge(S.vc, n_lists)
+    for k in range(8):
+        sy.dma_start(T.offs[16 * k:16 * k + 16, :], pa(T.offl)).then_inc(S.rep, 16)
+    sy.dma_start(T.vs[:, :], T.v[:, :]).then_inc(S.luv, 16)
+    sy.dma_start(T.us[:, :], T.u[:, :]).then_inc(S.luv, 16)
+    for k in range(8):
+        sy.dma_start(T.pfs[16 * k:16 * k + 16, :], T.pf[:, :]).then_inc(S.lpl, 16)
+        sy.dma_start(T.pgs[16 * k:16 * k + 16, :], T.pg[:, :]).then_inc(S.lpl, 16)
+
+    te.wait_ge(S.qx, 1)
+    for i in range(4):
+        if i < 3:
+            te.wait_ge((S.qa0, S.qa1, S.qa2)[i], 1)
+        te.matmul_mx(T.z[:, 512 * i:512 * i + NT], T.aq[:, 128 * i:128 * i + 128], T.ap_[:, 128 * i:128 * i + 128],
+                     T.xq[:, :], T.xp[:, :], True, True).then_inc(S["mm%d" % i], 1)
+        s.wait_ge(S["mm%d" % i], 1)
+        s.activation(T.win[:, i * W:i * W + NT], T.z[:, 512 * i:512 * i + NT], RELU, scale=0.05).then_inc(
+            S["rl%d" % i], 1)
+
+    def mask(k):
+        return T.mk[:, M_LEV + (k - 1) * NB:M_LEV + k * NB]
+
+    def build_one(i):
+        w, m4 = i * W, T.mk[:, 0:NT]
+        v.wait_ge(S["rl%d" % i], 1)
+        v.tensor_tensor_scan(T.win[:, w + O_P4:w + O_P4 + NT], m4, T.win[:, w:w + NT], 0.0, MUL, MAX).then_inc(
+            S["p4_%d" % i], 1)
+        v.tensor_tensor_scan(rev(T.win, w + O_S4, w + O_S4 + NT), m4, rev(T.win, w, w + NT), 0.0, MUL, MAX).then_inc(
+            S["bd%d" % i], 1)
+
+    def build_two(i):
+        w, bd = i * W, S["bd%d" % i]
+        v.wait_ge(S["p4_%d" % i], 1)
+        fwd = T.win[:, w + O_P4 + 3:w + O_P4 + NT:4]
+        bwd = rev(T.win, w + O_P4 + 3, w + O_P4 + NT, 4)
+        v.tensor_copy(T.win[:, w + BD:w + BD + NB], fwd).then_inc(bd, 1)
+        for k in range(1, LEV + 1):
+            p, q = w + BD - k * NB, w + BD + k * NB
+            v.tensor_tensor_scan(T.win[:, p:p + NB], mask(k), fwd, 0.0, MUL, MAX).then_inc(bd, 1)
+            v.tensor_tensor_scan(rev(T.win, q, q + NB), mask(k), bwd, 0.0, MUL, MAX).then_inc(bd, 1)
+
+    n_build = 2 + 2 * LEV
+
+    def off(p, a, b):
+        return T.offs[:, p * LC + a // 16:p * LC + b // 16]
+
+    def win(i):
+        return T.win[:, i * W:(i + 1) * W]
+
+    def gather(i, a, b, sem):
+        for p in range(3):
+            s.activation(T["g%d" % i][:, 3 * a + p:3 * b:3], win(i).indirect(off(p, a, b)), COPY).then_inc(sem, 1)
+
+    def merge(i, a, b, got, mid, out):
+        G, M = T["g%d" % i], T["m%d" % i]
+        v.wait_ge(got, 3)
+        v.tensor_tensor_scan(M[:, 3 * a:3 * b], T.mk[:, M_TRI:M_TRI + 3 * (b - a)], G[:, 3 * a:3 * b], 0.0,
+                             MUL, MAX).then_inc(mid, 1)
+        v.wait_ge(mid, 1)
+        v.tensor_tensor(T.tile[:, 4 * a + i:4 * b:4], win(i).indirect(off(3, a, b)), M[:, 3 * a + 2:3 * b:3],
+                        MAX).then_inc(out, 1)
+
+    s.wait_ge(S.rep, 128)
+    for i in range(4):
+        s.wait_ge(S["bd%d" % i], n_build)
+        if i < 3:
+            gather(i, 0, SL, S["ga%d" % i])
+        else:
+            gather(i, fs, fs + HALF, S.g3f)
+            gather(i, ns, ns + HALF, S.g3n)
+
+    v.wait_ge(S.vm, n_masks)
+    build_one(0)
+    quant_a(256, 512, S.la2, S.qa2)
+    build_two(0)
+    for i in (1, 2):
+        build_one(i)
+        build_two(i)
+    v.wait_ge(S.rep, 128)
+    merge(0, 0, SL, S.ga0, S.me0, S.tl)
+    build_one(3)
+    build_two(3)
+    merge(1, 0, SL, S.ga1, S.me1, S.tl)
+    merge(2, 0, SL, S.ga2, S.me2, S.tl)
+    merge(3, fs, fs + HALF, S.g3f, S.m3f, S.tlf)
+    v.wait_ge(S.tl, 3)
+    v.wait_ge(S.tlf, 1)
+    v.quantize_mx(T.fq[:, :], T.fp[:, :], T.tile[:, 4 * fs:4 * (fs + HALF)]).then_inc(S.qf, 1)
+    merge(3, ns, ns + HALF, S.g3n, S.m3n, S.tln)
+    v.wait_ge(S.tln, 1)
+    v.quantize_mx(T.nq[:, :], T.np_[:, :], T.tile[:, 4 * ns:4 * (ns + HALF)]).then_inc(S.qn, 1)
+
+    n_loc = [0]
+
+    def send(isfar, mine, src_q, src_p, dst_q, dst_p, arr):
+        dests = [q for q in mine if q != rank]
+        masks = engine_plan(core, [cores[q] for q in dests], topo)
+        for codes in (True, False):
+            tr = []
+            for q in dests:
+                a = mine.index(q) * CAPP
+                b = group(cores[q], isfar).index(rank) * CAPP
+                rid, pid, _se = topo.addr(cores[q])
+                m = 0
+                for e in masks[cores[q]]:
+                    m |= 1 << e
+                    n_loc[0] += 1
+                if codes:
+                    src, dst = src_q[:, a:a + CAPP].bitcast(dt.uint8), dst_q[:, b:b + CAPP].bitcast(dt.uint8)
+                else:
+                    src, dst = src_p[:, a:a + CAPP], dst_p[:, b:b + CAPP]
+                tr.append(RemoteDMATransfer(dst_ids=[DstId(rid=rid, pnc=pid)], dma_engine_mask=m, remote_sem=arr,
+                                            src=src, dst=dst))
+            g.remote_dma_fused(tr, local_sem=S.loc)
+
+    def arrivals(isfar, mine):
+        n = 0
+        for q in mine:
+            if q != rank:
+                peers = [cores[p] for p in group(cores[q], isfar) if p != q]
+                n += 2 * len(engine_plan(cores[q], peers, topo)[core])
+        return n
+
+    g.wait_ge(S.qf, 1)
+    send(True, far, T.fq, T.fp, T.rfq, T.rfp, S.arrf)
+    g.wait_ge(S.qn, 1)
+    send(False, near, T.nq, T.np_, T.rnq, T.rnp, S.arrn)
+    g.wait_ge(S.loc, n_loc[0])
+
+    me = near.index(rank) * CAPP
+    sy.wait_ge(S.qn, 1)
+    sy.dma_start(T.rnq[:, me:me + CAPP].bitcast(dt.uint8), T.nq[:, me:me + CAPP].bitcast(dt.uint8)).then_inc(S.own, 16)
+    sy.dma_start(T.rnp[:, me:me + CAPP], T.np_[:, me:me + CAPP]).then_inc(S.own, 16)
+
+    v.wait_ge(S.luv, 32)
+    v.quantize_mx(T.vq[:, :], T.vp[:, :], T.vs[:, :]).then_inc(S.quv, 1)
+    v.quantize_mx(T.uq[:, :], T.up[:, :], T.us[:, :]).then_inc(S.quv, 1)
+    v.wait_ge(S.lpl, 256)
+    done(v.tensor_scalar(T.pgt[:, :], T.pgs[:, :], 0.0, float(ZCOL + 1), LT, MUL))
+    v.tensor_copy(T.pfo[:, :], T.pfs[:, :]).then_inc(S.pl, 1)
+    sync_v()
+    done(v.tensor_tensor(T.pgn[:, :], T.pgs[:, :], T.pgt[:, :], ADD))
+    sync_v()
+    v.tensor_copy(T.pgo[:, :], T.pgn[:, :]).then_inc(S.pl, 1)
+    v.wait_ge(S.zero, 1)
+
+    te.wait_ge(S.quv, 2)
+    for k, (arr, n, cq, cp, first, sv, su) in enumerate((
+            (S.arrf, arrivals(True, far), T.rfq, T.rfp, fs, S.mfv, S.mfu),
+            (S.arrn, arrivals(False, near), T.rnq, T.rnp, ns, S.mnv, S.mnu))):
+        bv, bu = 2048 + 1024 * k, 2560 + 1024 * k
+        te.wait_ge(arr, n)
+        if k:
+            te.wait_ge(S.own, 32)
+        te.matmul_mx(T.z[:, bv:bv + HALF], T.vq[:, :], T.vp[:, :], cq[:, :], cp[:, :], True, True).then_inc(sv, 1)
+        te.matmul_mx(T.z[:, bu:bu + HALF], T.uq[:, :], T.up[:, :], cq[:, :], cp[:, :], True, True).then_inc(su, 1)
+        s.wait_ge(sv, 1)
+        s.activation(T.zv[:, first:first + HALF], T.z[:, bv:bv + HALF], COPY).then_inc(S.zvs, 1)
+        v.wait_ge(su, 1)
+        v.tensor_copy(T.zu[:, first:first + HALF], T.z[:, bu:bu + HALF]).then_inc(S.zus, 1)
+
+    h, hc = P // 2, P // 32
+    s.wait_ge(S.pl, 2)
+    s.wait_ge(S.zvs, 2)
+    v.wait_ge(S.pl, 2)
+    v.wait_ge(S.zus, 2)
+    for k in range(2):
+        gy, yy = (S.gy0, S.gy1)[k], (S.y0, S.y1)[k]
+        s.activation(T.gy[:, k * h:k * h + h], T.zv[:, :].indirect(T.pfo[:, k * hc:k * hc + hc]), COPY).then_inc(gy, 1)
+        v.wait_ge(gy, 1)
+        v.tensor_tensor(T.ys[:, k * h:k * h + h], T.zu[:, :].indirect(T.pgo[:, k * hc:k * hc + hc]),
+                        T.gy[:, k * h:k * h + h], ADD).then_inc(yy, 1)
+        sy.wait_ge(yy, 1)
+        sy.dma_start(T.y[:, k * h:k * h + h], T.ys[:, k * h:k * h + h]).then_inc(S.yo, 16)
+    sy.wait_ge(S.yo, 32)

@@ -4,16 +4,22 @@ from concourse.mybir import dt, AluOpType, ActivationFunctionType
 N, CAPP, NT, P = 8, 48, 512, 256
 SL = N * CAPP
 LC = SL // 16
-NB = NT // 4
-LEV = NB.bit_length() - 2
-O_H, O_S4, O_P4 = 0, NT, 2 * NT
-BD = 3 * NT + LEV * NB
-W = BD + (LEV + 1) * NB
 HALF = SL // 2
-M_LEV = NT
-M_TRI = M_LEV + LEV * NB
-M_ALL = M_TRI + 3 * SL
+B1, B2 = 2, 5
+W1, W2 = 1 << B1, 1 << B2
+N1, N2 = NT // W1, NT // W2
+PER = W2 // W1
+O_S2, O_S1, O_H, O_P1, O_P2 = 0, NT, 2 * NT, 3 * NT, 4 * NT
+W = 5 * NT
+PH = 2 * NT
+WR = PH + (PER - 2) * NT
+ZERO = NT + 7
+K1, K2, K8, K16 = 0, NT, 2 * NT, 3 * NT + PER
+KALL = K16 + 5 * N2
+TRI, PAIR = 0, 3 * HALF
+KG = 5 * HALF
 ZCOL = SL
+BY_V = (2, 3)
 
 SCRATCH = {
     "xs": ("sbuf", [128, 4 * NT], "bfloat16"),
@@ -30,7 +36,11 @@ SCRATCH = {
     "vp": ("sbuf", [128, 128], "uint8"),
     "z": ("psum", [128, 4096], "float32"),
     "win": ("sbuf", [128, 4 * W], "bfloat16"),
-    "mk": ("sbuf", [128, M_ALL], "bfloat16"),
+    "runs": ("sbuf", [128, WR], "bfloat16"),
+    "d1": ("sbuf", [128, 4 * N1], "bfloat16"),
+    "d2": ("sbuf", [128, 4 * N2], "bfloat16"),
+    "mk": ("sbuf", [128, KALL], "bfloat16"),
+    "mg": ("sbuf", [128, KG], "bfloat16"),
     "tile": ("sbuf", [128, 4 * SL], "bfloat16"),
     "fq": ("sbuf", [128, HALF], "float8_e4m3fn_x4"),
     "fp": ("sbuf", [128, HALF], "uint8"),
@@ -44,32 +54,29 @@ SCRATCH = {
     "zu": ("sbuf", [128, SL + 16], "float32"),
     "gy": ("sbuf", [128, P], "float32"),
     "ys": ("sbuf", [128, P], "float32"),
-    "offs": ("sbuf", [128, 4 * LC], "uint16"),
-    "offl": ("sbuf", [128, 4 * LC], "uint16"),
-    "los": ("sbuf", [128, LC], "int32"),
+    "offs": ("sbuf", [128, 2 * LC], "uint16"),
+    "offr": ("sbuf", [128, LC], "uint16"),
+    "offsl": ("sbuf", [128, 2 * LC], "uint16"),
+    "offrl": ("sbuf", [128, LC], "uint16"),
+    "l_x": ("sbuf", [128, 4 * LC], "int32"),
     "lns": ("sbuf", [128, LC], "int32"),
-    "l_t": ("sbuf", [128, LC], "int32"),
-    "l_lr": ("sbuf", [128, 2 * LC], "int32"),
-    "l_q": ("sbuf", [128, 2 * LC], "int32"),
-    "l_12": ("sbuf", [128, 2 * LC], "int32"),
-    "l_ab": ("sbuf", [128, 2 * LC], "int32"),
-    "l_ad": ("sbuf", [128, 2 * LC], "int32"),
-    "l_cr": ("sbuf", [128, LC], "int32"),
-    "l_c12": ("sbuf", [128, 2 * LC], "int32"),
-    "l_mm": ("sbuf", [128, 2 * LC], "int32"),
-    "l_mid": ("sbuf", [128, 2 * LC], "int32"),
-    "l_sa": ("sbuf", [128, LEV * LC], "int32"),
-    "l_sb": ("sbuf", [128, LEV * LC], "int32"),
-    "l_ne": ("sbuf", [128, LEV * LC], "int32"),
-    "l_am": ("sbuf", [128, 2 * LC], "int32"),
-    "l_amm": ("sbuf", [128, 2 * LC], "int32"),
-    "l_amp": ("sbuf", [128, 2 * LC], "int32"),
-    "l_w": ("sbuf", [128, 2 * LC], "int32"),
-    "l_e": ("sbuf", [128, 3 * LC], "int32"),
-    "l_f": ("sbuf", [128, LC], "int32"),
-    "l_k": ("sbuf", [128, LC], "int32"),
-    "l_kw": ("sbuf", [128, 2 * LC], "int32"),
-    "l_o": ("sbuf", [128, 4 * LC], "int32"),
+    "l_e": ("sbuf", [128, LC], "int32"),
+    "l_v1": ("sbuf", [128, 4 * LC], "int32"),
+    "l_v2": ("sbuf", [128, 4 * LC], "int32"),
+    "l_d": ("sbuf", [128, 4 * LC], "int32"),
+    "l_u": ("sbuf", [128, 4 * LC], "int32"),
+    "l_c": ("sbuf", [128, 2 * LC], "int32"),
+    "l_g": ("sbuf", [128, 4 * LC], "int32"),
+    "l_o": ("sbuf", [128, 2 * LC], "int32"),
+    "l_pm": ("sbuf", [128, LC], "int32"),
+    "l_hi": ("sbuf", [128, LC], "int32"),
+    "l_q8": ("sbuf", [128, LC], "int32"),
+    "l_pm5": ("sbuf", [128, LC], "int32"),
+    "l_hi5": ("sbuf", [128, LC], "int32"),
+    "l_f1": ("sbuf", [128, LC], "int32"),
+    "l_fp": ("sbuf", [128, 2 * LC], "int32"),
+    "l_m": ("sbuf", [128, 2 * LC], "int32"),
+    "l_r": ("sbuf", [128, LC], "int32"),
     "pfs": ("sbuf", [128, P // 16], "int32"),
     "pgs": ("sbuf", [128, P // 16], "int32"),
     "pgt": ("sbuf", [128, P // 16], "int32"),
@@ -78,24 +85,25 @@ SCRATCH = {
     "pgo": ("sbuf", [128, P // 16], "uint16"),
 }
 for _i in range(4):
-    SCRATCH["g%d" % _i] = ("sbuf", [128, 3 * SL], "bfloat16")
-    SCRATCH["m%d" % _i] = ("sbuf", [128, 3 * SL], "bfloat16")
+    _k = 2 if _i in BY_V else 3
+    SCRATCH["g%d" % _i] = ("sbuf", [128, _k * SL], "bfloat16")
+    SCRATCH["m%d" % _i] = ("sbuf", [128, _k * SL], "bfloat16")
 
-SEMAPHORES = (["lst", "lx", "la0", "la1", "la2", "luv", "lpl", "rep", "vm", "vc", "qx", "qa0", "qa1", "qa2", "quv",
+SEMAPHORES = (["lst", "lx0", "lx1", "la0", "la1", "la2", "luv", "lpl", "rep", "repr_", "o1", "o2", "vm", "vc",
+               "qx", "qa0", "qa1", "qa2", "quv", "gi", "gm", "d1s", "d2s", "rs",
                "qf", "qn", "zero", "pl", "own", "arrf", "arrn", "loc", "mfv", "mfu", "mnv", "mnu", "zvs", "zus",
-               "gy0", "gy1", "y0", "y1", "yo", "tl", "tlf", "tln", "g3f", "g3n", "m3f", "m3n"]
-              + ["mm%d" % i for i in range(4)] + ["rl%d" % i for i in range(4)]
-              + ["p4_%d" % i for i in range(4)] + ["bd%d" % i for i in range(4)]
-              + ["ga%d" % i for i in range(3)] + ["me%d" % i for i in range(3)])
+               "gy0", "gy1", "y0", "y1", "yo", "tlf", "tln"]
+              + ["%s%d" % (_n, _i) for _i in range(4)
+                 for _n in ("mm", "rl", "p1_", "p2_", "ss", "ge", "grf", "grn", "mef", "men")])
 
 ADD, SUB, MUL, MAX, MIN = AluOpType.add, AluOpType.subtract, AluOpType.mult, AluOpType.max, AluOpType.min
-GE, GT, LT, NEQ = AluOpType.is_ge, AluOpType.is_gt, AluOpType.is_lt, AluOpType.not_equal
-SHR = AluOpType.arith_shift_right
+GE, GT, LT, NEQ, EQ = AluOpType.is_ge, AluOpType.is_gt, AluOpType.is_lt, AluOpType.not_equal, AluOpType.is_equal
+SHR, AND = AluOpType.arith_shift_right, AluOpType.bitwise_and
 RELU, COPY = ActivationFunctionType.Relu, ActivationFunctionType.Copy
 
 
-def rev(t, lo, hi, step=1):
-    return t[:, hi - 1:(lo - 1 if lo > 0 else None):-step]
+def rev(t, lo, hi):
+    return t[:, hi - 1:(lo - 1 if lo > 0 else None):-1]
 
 
 def engine_plan(core, dests, topo):
@@ -104,15 +112,12 @@ def engine_plan(core, dests, topo):
     per = 1
     while 2 * per * len(off) <= len(pool):
         per *= 2
-    masks, used = {}, []
+    masks = {}
     for k, d in enumerate(off):
         masks[d] = pool[k * per:(k + 1) * per]
-        used += masks[d]
     for d in dests:
         if d not in masks:
-            free = [e for e in topo.engines(core, d) if e not in pool]
-            masks[d] = free[:2]
-            used += masks[d]
+            masks[d] = [e for e in topo.engines(core, d) if e not in pool][:2]
     return masks
 
 
@@ -131,23 +136,26 @@ def rank_program(g, core, T, topo):
 
     far, near = group(core, True), group(core, False)
     fs, ns = far[0] * CAPP, near[0] * CAPP
+    L, L2, L3, L4 = LC, 2 * LC, 3 * LC, 4 * LC
 
-    s.dma_start(T.los[0:16, :], T.lo[:, :]).then_inc(S.lst, 16)
+    s.dma_start(T.l_x[0:16, 0:L], T.lo[:, :]).then_inc(S.lst, 16)
     sy.dma_start(T.lns[0:16, :], T.ln[:, :]).then_inc(S.lst, 16)
-    sy.dma_start(T.xs[:, :], T.x[:, :]).then_inc(S.lx, 16)
-    sy.dma_start(T.as_[:, 0:512], T.a[:, 0:512]).then_inc(S.la0, 16)
+    sy.dma_start(T.xs[:, 0:2 * NT], T.x[:, 0:2 * NT]).then_inc(S.lx0, 16)
+    s.dma_start(T.as_[:, 0:512], T.a[:, 0:512]).then_inc(S.la0, 16)
+    sy.dma_start(T.xs[:, 2 * NT:4 * NT], T.x[:, 2 * NT:4 * NT]).then_inc(S.lx1, 16)
     sy.dma_start(T.as_[:, 512:1024], T.a[:, 512:1024]).then_inc(S.la1, 16)
     sy.dma_start(T.as_[:, 1024:2048], T.a[:, 1024:2048]).then_inc(S.la2, 16)
 
-    v.memset(T.mk[:, :], 1.0).then_inc(S.vm, 1)
+    g.iota(T.mg[:, :], [[0, KG]], 1, 0, allow_small_or_imprecise_dtypes=True).then_inc(S.gi, 1)
+    g.wait_ge(S.gi, 1)
+    for o, k in ((TRI, 3), (PAIR, 2)):
+        m = T.mg[:, o:o + k * HALF]
+        g.affine_select(m, m, [[0, HALF], [1, k]], NEQ, 0.0, 0, 0).then_inc(S.gm, 1)
+
+    v.memset(T.mk[:, K1:K1 + NT], 1.0).then_inc(S.vm, 1)
     v.memset(T.zu[:, ZCOL:ZCOL + 16], 0.0).then_inc(S.zero, 1)
     v.wait_ge(S.vm, 1)
-    v.memset(T.mk[:, 0:NT:4], 0.0).then_inc(S.vm, 1)
-    for k in range(1, LEV + 1):
-        b = M_LEV + (k - 1) * NB
-        v.memset(T.mk[:, b:b + NB:1 << k], 0.0).then_inc(S.vm, 1)
-    v.memset(T.mk[:, M_TRI:M_ALL:3], 0.0).then_inc(S.vm, 1)
-    n_masks = LEV + 3
+    v.memset(T.mk[:, K1:K1 + NT:W1], 0.0).then_inc(S.vm, 1)
 
     cnt = [0]
 
@@ -161,162 +169,201 @@ def rank_program(g, core, T, topo):
     def pa(t, a=None, b=None):
         return t[0:16, :] if a is None else t[0:16, a:b]
 
-    L, L2 = LC, 2 * LC
-
-    def lists_one():
-        v.wait_ge(S.lst, 32)
-        done(v.tensor_tensor(pa(T.l_t), pa(T.los), pa(T.lns), ADD))
-        done(v.tensor_scalar(pa(T.l_lr, 0, L), pa(T.los), 0.0, None, MAX))
-        sync_v()
-        done(v.tensor_scalar(pa(T.l_lr, L, L2), pa(T.l_t), -1.0, 0.0, ADD, MAX))
-        sync_v()
-        done(v.tensor_scalar(pa(T.l_q), pa(T.l_lr), 2, None, SHR))
-        done(v.tensor_scalar(pa(T.l_12, 0, L), pa(T.l_lr, 0, L), 1.0, None, ADD))
-        done(v.tensor_scalar(pa(T.l_12, L, L2), pa(T.l_lr, 0, L), 2.0, None, ADD))
-        sync_v()
-        done(v.tensor_scalar(pa(T.l_ab, 0, L), pa(T.l_q, 0, L), 1.0, None, ADD))
-        done(v.tensor_scalar(pa(T.l_ab, L, L2), pa(T.l_q, L, L2), -1.0, None, ADD))
-        done(v.tensor_scalar(pa(T.l_ad, 0, L), pa(T.l_q, 0, L), float(BD + 1), None, ADD))
-        done(v.tensor_scalar(pa(T.l_ad, L, L2), pa(T.l_q, L, L2), float(BD - 1), None, ADD))
-        done(v.tensor_tensor(pa(T.l_cr), pa(T.l_q, L, L2), pa(T.l_q, 0, L), GT))
-        done(v.tensor_tensor(pa(T.l_mm, 0, L), pa(T.l_12, 0, L), pa(T.l_lr, L, L2), MIN))
-        done(v.tensor_tensor(pa(T.l_mm, L, L2), pa(T.l_12, L, L2), pa(T.l_lr, L, L2), MIN))
-        sync_v()
-        for j in range(1, LEV + 1):
-            done(v.tensor_scalar(pa(T.l_sa, (j - 1) * L, j * L), pa(T.l_ab, 0, L), j, None, SHR))
-            done(v.tensor_scalar(pa(T.l_sb, (j - 1) * L, j * L), pa(T.l_ab, L, L2), j, None, SHR))
-        done(v.tensor_tensor(pa(T.l_mid, 0, L), pa(T.l_ab, L, L2), pa(T.l_ab, 0, L), GE))
-        done(v.tensor_tensor(pa(T.l_mid, L, L2), pa(T.l_ab, L, L2), pa(T.l_ab, 0, L), GE))
-        done(v.tensor_scalar(pa(T.l_c12, 0, L), pa(T.l_cr), float(O_S4), None, MUL))
-        done(v.tensor_scalar(pa(T.l_c12, L, L2), pa(T.l_cr), float(O_P4), None, MUL))
-        done(v.tensor_tensor(pa(T.l_am), pa(T.l_ad), pa(T.l_mm), SUB))
-
-    def lists_two():
-        sync_v()
-        done(v.tensor_tensor(pa(T.l_ne), pa(T.l_sa), pa(T.l_sb), NEQ))
-        done(v.tensor_tensor(pa(T.l_amm), pa(T.l_am), pa(T.l_mid), MUL))
-        done(v.tensor_tensor(pa(T.l_o, 0, L2), pa(T.l_lr), pa(T.l_c12), ADD))
-        done(v.tensor_scalar(pa(T.l_w, 0, L), pa(T.l_mid, 0, L), float(NB), None, MUL))
-        done(v.tensor_scalar(pa(T.l_w, L, L2), pa(T.l_mid, L, L2), float(-NB), None, MUL))
-        sync_v()
-        done(v.tensor_tensor(pa(T.l_e), pa(T.l_ne, 0, 3 * L), pa(T.l_ne, 3 * L, 6 * L), ADD))
-        done(v.tensor_tensor(pa(T.l_amp), pa(T.l_amm), pa(T.l_mm), ADD))
-        sync_v()
-        done(v.tensor_tensor(pa(T.l_f), pa(T.l_e, 0, L), pa(T.l_e, L, L2), ADD))
-        sync_v()
-        done(v.tensor_tensor(pa(T.l_k), pa(T.l_f), pa(T.l_e, L2, 3 * L), ADD))
-        sync_v()
-        done(v.tensor_tensor(pa(T.l_kw, 0, L), pa(T.l_k), pa(T.l_w, 0, L), MUL))
-        done(v.tensor_tensor(pa(T.l_kw, L, L2), pa(T.l_k), pa(T.l_w, L, L2), MUL))
-        sync_v()
-        done(v.tensor_tensor(pa(T.l_o, L2, 4 * L), pa(T.l_kw), pa(T.l_amp), ADD))
-        sync_v()
-        done(v.tensor_copy(pa(T.offl), pa(T.l_o)))
-
-    lists_one()
+    v.wait_ge(S.lst, 32)
+    done(v.tensor_tensor(pa(T.l_x, L2, L3), pa(T.l_x, 0, L), pa(T.lns), ADD))
+    done(v.tensor_scalar(pa(T.l_x, L, L2), pa(T.l_x, 0, L), -1.0, None, ADD))
+    done(v.tensor_scalar(pa(T.l_e), pa(T.l_x, 0, L), float(O_H), None, ADD))
+    sync_v()
+    done(v.tensor_scalar(pa(T.l_x, L3, L4), pa(T.l_x, L2, L3), -1.0, None, ADD))
+    sync_v()
+    done(v.tensor_scalar(pa(T.l_v1), pa(T.l_x), B1, None, SHR))
+    done(v.tensor_scalar(pa(T.l_v2), pa(T.l_x), B2, None, SHR))
+    sync_v()
+    done(v.tensor_tensor(pa(T.l_d, 0, L2), pa(T.l_v1, L2, L4), pa(T.l_v1, 0, L2), SUB))
+    done(v.tensor_tensor(pa(T.l_d, L2, L4), pa(T.l_v2, L2, L4), pa(T.l_v2, 0, L2), SUB))
+    done(v.tensor_scalar(pa(T.l_pm), pa(T.l_v1, 0, L), PER - 1, None, AND))
+    done(v.tensor_scalar(pa(T.l_hi), pa(T.l_v2, 0, L), 3, None, SHR))
+    done(v.tensor_scalar(pa(T.l_q8), pa(T.l_v2, L2, L3), 8.0, None, MUL))
+    sync_v()
+    done(v.tensor_scalar(pa(T.l_u), pa(T.l_d), 1.0, float(NT), MIN, MUL))
+    done(v.tensor_scalar(pa(T.l_g, 0, L3), pa(T.l_d, 0, L3), 2.0, None, GE))
+    sync_v()
+    done(v.tensor_tensor(pa(T.l_c), pa(T.l_u, 0, L2), pa(T.l_u, L2, L4), ADD))
+    done(v.tensor_scalar(pa(T.l_pm5), pa(T.l_pm), float(NT), float(PH - 1 - ZERO), MUL, ADD))
+    done(v.tensor_scalar(pa(T.l_hi5), pa(T.l_hi), float(NT - 8), float(-8 - ZERO), MUL, ADD))
+    done(v.tensor_tensor(pa(T.l_f1), pa(T.l_q8), pa(T.l_v2, 0, L), ADD))
+    sync_v()
+    done(v.tensor_tensor(pa(T.l_o, 0, L), pa(T.l_e), pa(T.l_c, 0, L), SUB))
+    done(v.tensor_tensor(pa(T.l_o, L, L2), pa(T.l_x, L3, L4), pa(T.l_c, L, L2), ADD))
+    done(v.tensor_tensor(pa(T.l_fp, 0, L), pa(T.l_f1), pa(T.l_hi5), ADD))
+    done(v.tensor_tensor(pa(T.l_fp, L, L2), pa(T.l_v1, L2, L3), pa(T.l_pm5), ADD))
+    done(v.tensor_tensor(pa(T.l_g, L3, L4), pa(T.l_g, 0, L), pa(T.l_u, L2, L3), GT))
+    sync_v()
+    v.tensor_copy(pa(T.offsl), pa(T.l_o)).then_inc(S.o1, 1)
+    done(v.tensor_tensor(pa(T.l_m), pa(T.l_fp), pa(T.l_g, L2, L4), MUL))
+    sync_v()
+    done(v.tensor_tensor(pa(T.l_r), pa(T.l_m, 0, L), pa(T.l_m, L, L2), ADD))
 
     def quant_a(lo, hi, load, q):
         v.wait_ge(load, 16)
         v.quantize_mx(T.aq[:, lo:hi], T.ap_[:, lo:hi], T.as_[:, 4 * lo:4 * hi]).then_inc(q, 1)
 
-    v.wait_ge(S.lx, 16)
-    v.quantize_mx(T.xq[:, :], T.xp[:, :], T.xs[:, :]).then_inc(S.qx, 1)
-    quant_a(0, 128, S.la0, S.qa0)
-    lists_two()
-    n_lists = cnt[0]
-    quant_a(128, 256, S.la1, S.qa1)
+    def quant_x(lo, hi, load):
+        v.wait_ge(load, 16)
+        v.quantize_mx(T.xq[:, lo:hi], T.xp[:, lo:hi], T.xs[:, 4 * lo:4 * hi]).then_inc(S.qx, 1)
 
-    sy.wait_ge(S.vc, n_lists)
+    quant_x(0, NT // 2, S.lx0)
+    quant_a(0, 128, S.la0, S.qa0)
+    quant_x(NT // 2, NT, S.lx1)
+    sync_v()
+    v.tensor_scalar(pa(T.offrl), pa(T.l_r), float(ZERO), None, ADD).then_inc(S.o2, 1)
+
+    v.memset(T.mk[:, K2:KALL], 1.0).then_inc(S.vm, 1)
+    v.memset(T.runs[:, ZERO:2 * NT:8], 0.0).then_inc(S.rs, 1)
+    quant_a(128, 256, S.la1, S.qa1)
+    v.wait_ge(S.vm, 3)
+    v.memset(T.mk[:, K2:K2 + NT:W2], 0.0).then_inc(S.vm, 1)
+    v.memset(T.mk[:, K8:K8 + NT + PER:PER], 0.0).then_inc(S.vm, 1)
+    v.memset(T.mk[:, K16:KALL:N2], 0.0).then_inc(S.vm, 1)
+
+    sy.wait_ge(S.o1, 1)
     for k in range(8):
-        sy.dma_start(T.offs[16 * k:16 * k + 16, :], pa(T.offl)).then_inc(S.rep, 16)
+        sy.dma_start(T.offs[16 * k:16 * k + 16, :], pa(T.offsl)).then_inc(S.rep, 16)
+    sy.wait_ge(S.o2, 1)
+    for k in range(8):
+        sy.dma_start(T.offr[16 * k:16 * k + 16, :], pa(T.offrl)).then_inc(S.repr_, 16)
     sy.dma_start(T.vs[:, :], T.v[:, :]).then_inc(S.luv, 16)
     sy.dma_start(T.us[:, :], T.u[:, :]).then_inc(S.luv, 16)
     for k in range(8):
         sy.dma_start(T.pfs[16 * k:16 * k + 16, :], T.pf[:, :]).then_inc(S.lpl, 16)
         sy.dma_start(T.pgs[16 * k:16 * k + 16, :], T.pg[:, :]).then_inc(S.lpl, 16)
 
-    te.wait_ge(S.qx, 1)
+    te.wait_ge(S.qx, 2)
     for i in range(4):
         if i < 3:
             te.wait_ge((S.qa0, S.qa1, S.qa2)[i], 1)
         te.matmul_mx(T.z[:, 512 * i:512 * i + NT], T.aq[:, 128 * i:128 * i + 128], T.ap_[:, 128 * i:128 * i + 128],
                      T.xq[:, :], T.xp[:, :], True, True).then_inc(S["mm%d" % i], 1)
+
+    def relu(i):
         s.wait_ge(S["mm%d" % i], 1)
-        s.activation(T.win[:, i * W:i * W + NT], T.z[:, 512 * i:512 * i + NT], RELU, scale=0.05).then_inc(
+        s.activation(T.win[:, i * W + O_H:i * W + O_H + NT], T.z[:, 512 * i:512 * i + NT], RELU, scale=0.05).then_inc(
             S["rl%d" % i], 1)
 
-    def mask(k):
-        return T.mk[:, M_LEV + (k - 1) * NB:M_LEV + k * NB]
+    def per(i):
+        return 2 if i in BY_V else 3
 
-    def build_one(i):
-        w, m4 = i * W, T.mk[:, 0:NT]
-        v.wait_ge(S["rl%d" % i], 1)
-        v.tensor_tensor_scan(T.win[:, w + O_P4:w + O_P4 + NT], m4, T.win[:, w:w + NT], 0.0, MUL, MAX).then_inc(
-            S["p4_%d" % i], 1)
-        v.tensor_tensor_scan(rev(T.win, w + O_S4, w + O_S4 + NT), m4, rev(T.win, w, w + NT), 0.0, MUL, MAX).then_inc(
-            S["bd%d" % i], 1)
+    def gather_p(i):
+        s.wait_ge(S["p1_%d" % i], 1)
+        s.wait_ge(S["p2_%d" % i], 1)
+        s.activation(T["g%d" % i][:, 1::per(i)], T.win[:, i * W + O_H:i * W + W].indirect(T.offs[:, L:L2]),
+                     COPY).then_inc(S["ge%d" % i], 1)
 
-    def build_two(i):
-        w, bd = i * W, S["bd%d" % i]
-        v.wait_ge(S["p4_%d" % i], 1)
-        fwd = T.win[:, w + O_P4 + 3:w + O_P4 + NT:4]
-        bwd = rev(T.win, w + O_P4 + 3, w + O_P4 + NT, 4)
-        v.tensor_copy(T.win[:, w + BD:w + BD + NB], fwd).then_inc(bd, 1)
-        for k in range(1, LEV + 1):
-            p, q = w + BD - k * NB, w + BD + k * NB
-            v.tensor_tensor_scan(T.win[:, p:p + NB], mask(k), fwd, 0.0, MUL, MAX).then_inc(bd, 1)
-            v.tensor_tensor_scan(rev(T.win, q, q + NB), mask(k), bwd, 0.0, MUL, MAX).then_inc(bd, 1)
+    def gather_s(i):
+        s.wait_ge(S["ss%d" % i], 2)
+        s.activation(T["g%d" % i][:, 0::per(i)], T.win[:, i * W:i * W + O_P1].indirect(T.offs[:, 0:L]),
+                     COPY).then_inc(S["ge%d" % i], 1)
 
-    n_build = 2 + 2 * LEV
+    def runs(i, a):
+        return T.runs[:, i * N1:WR].indirect(T.offr[:, a // 16:(a + HALF) // 16])
 
-    def off(p, a, b):
-        return T.offs[:, p * LC + a // 16:p * LC + b // 16]
-
-    def win(i):
-        return T.win[:, i * W:(i + 1) * W]
-
-    def gather(i, a, b, sem):
-        for p in range(3):
-            s.activation(T["g%d" % i][:, 3 * a + p:3 * b:3], win(i).indirect(off(p, a, b)), COPY).then_inc(sem, 1)
-
-    def merge(i, a, b, got, mid, out):
-        G, M = T["g%d" % i], T["m%d" % i]
-        v.wait_ge(got, 3)
-        v.tensor_tensor_scan(M[:, 3 * a:3 * b], T.mk[:, M_TRI:M_TRI + 3 * (b - a)], G[:, 3 * a:3 * b], 0.0,
-                             MUL, MAX).then_inc(mid, 1)
-        v.wait_ge(mid, 1)
-        v.tensor_tensor(T.tile[:, 4 * a + i:4 * b:4], win(i).indirect(off(3, a, b)), M[:, 3 * a + 2:3 * b:3],
-                        MAX).then_inc(out, 1)
-
+    relu(0)
+    relu(1)
     s.wait_ge(S.rep, 128)
-    for i in range(4):
-        s.wait_ge(S["bd%d" % i], n_build)
-        if i < 3:
-            gather(i, 0, SL, S["ga%d" % i])
-        else:
-            gather(i, fs, fs + HALF, S.g3f)
-            gather(i, ns, ns + HALF, S.g3n)
+    gather_p(0)
+    relu(2)
+    relu(3)
+    gather_s(0)
+    for i in (1, 2, 3):
+        gather_p(i)
+        gather_s(i)
+    n_runs = 1 + (PER - 2) + (N2 - 1)
+    s.wait_ge(S.rs, n_runs)
+    s.wait_ge(S.repr_, 128)
+    for a, sem in ((fs, "grf%d"), (ns, "grn%d")):
+        for i in range(4):
+            if i not in BY_V:
+                s.activation(T["g%d" % i][:, 3 * a + 2:3 * (a + HALF):3], runs(i, a), COPY).then_inc(S[sem % i], 1)
 
-    v.wait_ge(S.vm, n_masks)
-    build_one(0)
+    for i in range(4):
+        for sem, o, w, n, d, ds in (("p1_%d", O_P1, W1, N1, T.d1, S.d1s), ("p2_%d", O_P2, W2, N2, T.d2, S.d2s)):
+            g.wait_ge(S[sem % i], 1)
+            b = i * W + o
+            g.affine_select(d[:, i * n:(i + 1) * n], T.win[:, b + w - 1:b + NT:w], [[0, n]], EQ, 0.0, 0, 0).then_inc(
+                ds, 1)
+
+    def build_p(i):
+        w = i * W
+        v.wait_ge(S["rl%d" % i], 1)
+        for o, k, sem in ((O_P1, K1, "p1_%d"), (O_P2, K2, "p2_%d")):
+            v.tensor_tensor_scan(T.win[:, w + o:w + o + NT], T.mk[:, k:k + NT], T.win[:, w + O_H:w + O_H + NT], 0.0,
+                                 MUL, MAX).then_inc(S[sem % i], 1)
+
+    def build_s(i):
+        w = i * W
+        for o, k in ((O_S1, K1), (O_S2, K2)):
+            v.tensor_tensor_scan(rev(T.win, w + o, w + o + NT), T.mk[:, k:k + NT],
+                                 rev(T.win, w + O_H, w + O_H + NT), 0.0, MUL, MAX).then_inc(S["ss%d" % i], 1)
+
+    v.wait_ge(S.vm, 6)
+    build_p(0)
     quant_a(256, 512, S.la2, S.qa2)
-    build_two(0)
-    for i in (1, 2):
-        build_one(i)
-        build_two(i)
-    v.wait_ge(S.rep, 128)
-    merge(0, 0, SL, S.ga0, S.me0, S.tl)
-    build_one(3)
-    build_two(3)
-    merge(1, 0, SL, S.ga1, S.me1, S.tl)
-    merge(2, 0, SL, S.ga2, S.me2, S.tl)
-    merge(3, fs, fs + HALF, S.g3f, S.m3f, S.tlf)
-    v.wait_ge(S.tl, 3)
-    v.wait_ge(S.tlf, 1)
-    v.quantize_mx(T.fq[:, :], T.fp[:, :], T.tile[:, 4 * fs:4 * (fs + HALF)]).then_inc(S.qf, 1)
-    merge(3, ns, ns + HALF, S.g3n, S.m3n, S.tln)
-    v.wait_ge(S.tln, 1)
-    v.quantize_mx(T.nq[:, :], T.np_[:, :], T.tile[:, 4 * ns:4 * (ns + HALF)]).then_inc(S.qn, 1)
+    build_s(0)
+    for i in (1, 2, 3):
+        build_p(i)
+        build_s(i)
+    v.wait_ge(S.d1s, 4)
+    for m in range(PER - 2):
+        k, o = K8 + PER - 1 - m, PH + m * NT
+        v.tensor_tensor_scan(T.runs[:, o:o + NT], T.mk[:, k:k + NT], T.d1[:, :], 0.0, MUL, MAX).then_inc(S.rs, 1)
+    v.wait_ge(S.d2s, 4)
+    for q in range(N2 - 1):
+        k, o = K16 + N2 - 1 - q, (q >> 3) * NT
+        v.tensor_tensor_scan(T.runs[:, o + (q & 7):o + NT:8], T.mk[:, k:k + 4 * N2], T.d2[:, :], 0.0,
+                             MUL, MAX).then_inc(S.rs, 1)
+
+    def scan(i, a, sem):
+        k = per(i)
+        m = (PAIR if k == 2 else TRI)
+        v.tensor_tensor_scan(T["m%d" % i][:, k * a:k * (a + HALF)], T.mg[:, m:m + k * HALF],
+                             T["g%d" % i][:, k * a:k * (a + HALF)], 0.0, MUL, MAX).then_inc(S[sem % i], 1)
+
+    def merged(i, a, sem, out):
+        k = per(i)
+        M = T["m%d" % i][:, k * a + k - 1:k * (a + HALF):k]
+        dst = T.tile[:, 4 * a + i:4 * (a + HALF):4]
+        v.wait_ge(S[sem % i], 1)
+        if k == 2:
+            v.tensor_tensor(dst, runs(i, a), M, MAX).then_inc(out, 1)
+        else:
+            v.tensor_copy(dst, M).then_inc(out, 1)
+
+    v.wait_ge(S.gm, 2)
+    v.wait_ge(S.ge2, 2)
+    scan(2, fs, "mef%d")
+    scan(2, ns, "men%d")
+    v.wait_ge(S.rs, n_runs)
+    v.wait_ge(S.repr_, 128)
+    merged(2, fs, "mef%d", S.tlf)
+    merged(2, ns, "men%d", S.tln)
+    v.wait_ge(S.ge3, 2)
+    scan(3, fs, "mef%d")
+    scan(3, ns, "men%d")
+    merged(3, fs, "mef%d", S.tlf)
+    for a, gr, me, tl in ((fs, "grf%d", "mef%d", S.tlf), (ns, "grn%d", "men%d", S.tln)):
+        for i in (0, 1):
+            v.wait_ge(S["ge%d" % i], 2)
+            v.wait_ge(S[gr % i], 1)
+            scan(i, a, me)
+        merged(0, a, me, tl)
+        if a == ns:
+            merged(3, ns, me, tl)
+        merged(1, a, me, tl)
+        v.wait_ge(tl, 4)
+        if a == fs:
+            v.quantize_mx(T.fq[:, :], T.fp[:, :], T.tile[:, 4 * fs:4 * (fs + HALF)]).then_inc(S.qf, 1)
+        else:
+            v.quantize_mx(T.nq[:, :], T.np_[:, :], T.tile[:, 4 * ns:4 * (ns + HALF)]).then_inc(S.qn, 1)
 
     n_loc = [0]
 

@@ -11,15 +11,19 @@ N1, N2 = NT // W1, NT // W2
 PER = W2 // W1
 O_S2, O_S1, O_H, O_P1, O_P2 = 0, NT, 2 * NT, 3 * NT, 4 * NT
 W = 5 * NT
-PH = 2 * NT
-WR = PH + (PER - 2) * NT
-ZERO = NT + 7
+ND = 4 * N2
+AGAIN = ND + 8
+D2 = AGAIN + ND
+PH = 8 * D2
+D1 = PH + (PER - 3) * NT
+WR = D1 + NT
+ZERO = 8 * AGAIN + 7
 K1, K2, K8, K16 = 0, NT, 2 * NT, 3 * NT + PER
-KALL = K16 + 5 * N2
+KALL = K16 + D2 + N2
 TRI, PAIR = 0, 3 * HALF
 KG = 5 * HALF
 ZCOL = SL
-BY_V = (2, 3)
+BY_V = (1, 2, 3)
 
 SCRATCH = {
     "xs": ("sbuf", [128, 4 * NT], "bfloat16"),
@@ -37,8 +41,7 @@ SCRATCH = {
     "z": ("psum", [128, 4096], "float32"),
     "win": ("sbuf", [128, 4 * W], "bfloat16"),
     "runs": ("sbuf", [128, WR], "bfloat16"),
-    "d1": ("sbuf", [128, 4 * N1], "bfloat16"),
-    "d2": ("sbuf", [128, 4 * N2], "bfloat16"),
+    "d2": ("sbuf", [128, D2], "bfloat16"),
     "mk": ("sbuf", [128, KALL], "bfloat16"),
     "mg": ("sbuf", [128, KG], "bfloat16"),
     "tile": ("sbuf", [128, 4 * SL], "bfloat16"),
@@ -89,12 +92,16 @@ for _i in range(4):
     SCRATCH["g%d" % _i] = ("sbuf", [128, _k * SL], "bfloat16")
     SCRATCH["m%d" % _i] = ("sbuf", [128, _k * SL], "bfloat16")
 
-SEMAPHORES = (["lst", "lx0", "lx1", "la0", "la1", "la2", "luv", "lpl", "rep", "repr_", "o1", "o2", "vm", "vc",
-               "qx", "qa0", "qa1", "qa2", "quv", "gi", "gm", "d1s", "d2s", "rs",
+STEPS = ["t", "l1", "e", "r", "v1", "v2", "d1", "d2", "pm", "u", "hi", "c", "g", "o0", "o1", "q8", "pm5", "hi5", "f1",
+         "gp", "f", "p", "m", "sum", "pgt", "pgn"]
+
+SEMAPHORES = (["lst", "lx0", "lx1", "la0", "la1", "la2", "luv", "lpl", "rep", "repr_", "o1", "o2", "vm",
+               "qx0", "qx1", "qa0", "qa1", "qa2", "quv", "gi", "gm", "d1s", "d2s", "rs", "mmh",
                "qf", "qn", "zero", "pl", "own", "arrf", "arrn", "loc", "mfv", "mfu", "mnv", "mnu", "zvs", "zus",
-               "gy0", "gy1", "y0", "y1", "yo", "tlf", "tln"]
+               "gy0", "gy1", "y0", "y1", "yo", "tlf", "tln", "grf", "grn"]
+              + ["k_%s" % _n for _n in STEPS]
               + ["%s%d" % (_n, _i) for _i in range(4)
-                 for _n in ("mm", "rl", "p1_", "p2_", "ss", "ge", "grf", "grn", "mef", "men")])
+                 for _n in ("mm", "rl", "p1_", "p2_", "ss", "ge", "mef", "men")])
 
 ADD, SUB, MUL, MAX, MIN = AluOpType.add, AluOpType.subtract, AluOpType.mult, AluOpType.max, AluOpType.min
 GE, GT, LT, NEQ, EQ = AluOpType.is_ge, AluOpType.is_gt, AluOpType.is_lt, AluOpType.not_equal, AluOpType.is_equal
@@ -137,12 +144,13 @@ def rank_program(g, core, T, topo):
     far, near = group(core, True), group(core, False)
     fs, ns = far[0] * CAPP, near[0] * CAPP
     L, L2, L3, L4 = LC, 2 * LC, 3 * LC, 4 * LC
+    XH = NT // 2
 
     s.dma_start(T.l_x[0:16, 0:L], T.lo[:, :]).then_inc(S.lst, 16)
     sy.dma_start(T.lns[0:16, :], T.ln[:, :]).then_inc(S.lst, 16)
-    sy.dma_start(T.xs[:, 0:2 * NT], T.x[:, 0:2 * NT]).then_inc(S.lx0, 16)
+    sy.dma_start(T.xs[:, 0:4 * XH], T.x[:, 0:4 * XH]).then_inc(S.lx0, 16)
     s.dma_start(T.as_[:, 0:512], T.a[:, 0:512]).then_inc(S.la0, 16)
-    sy.dma_start(T.xs[:, 2 * NT:4 * NT], T.x[:, 2 * NT:4 * NT]).then_inc(S.lx1, 16)
+    sy.dma_start(T.xs[:, 4 * XH:4 * NT], T.x[:, 4 * XH:4 * NT]).then_inc(S.lx1, 16)
     sy.dma_start(T.as_[:, 512:1024], T.a[:, 512:1024]).then_inc(S.la1, 16)
     sy.dma_start(T.as_[:, 1024:2048], T.a[:, 1024:2048]).then_inc(S.la2, 16)
 
@@ -152,79 +160,80 @@ def rank_program(g, core, T, topo):
         m = T.mg[:, o:o + k * HALF]
         g.affine_select(m, m, [[0, HALF], [1, k]], NEQ, 0.0, 0, 0).then_inc(S.gm, 1)
 
-    v.memset(T.mk[:, K1:K1 + NT], 1.0).then_inc(S.vm, 1)
-    v.memset(T.zu[:, ZCOL:ZCOL + 16], 0.0).then_inc(S.zero, 1)
+    v.memset(T.mk[:, :], 1.0).then_inc(S.vm, 1)
+    v.memset(T.runs[:, 8 * ND + 7:PH:8], 0.0).then_inc(S.rs, 1)
+    v.memset(T.d2[:, ND:AGAIN], 0.0).then_inc(S.zero, 1)
     v.wait_ge(S.vm, 1)
-    v.memset(T.mk[:, K1:K1 + NT:W1], 0.0).then_inc(S.vm, 1)
+    for b, e, w in ((K1, K2, W1), (K2, K8, W2), (K8, K16, PER), (K16, KALL, N2)):
+        v.memset(T.mk[:, b:e:w], 0.0).then_inc(S.vm, 1)
 
-    cnt = [0]
+    def op(name, ins):
+        ins.then_inc(S["k_" + name], 1)
 
-    def done(ins):
-        ins.then_inc(S.vc, 1)
-        cnt[0] += 1
-
-    def sync_v():
-        v.wait_ge(S.vc, cnt[0])
+    def need(*names):
+        for n in names:
+            v.wait_ge(S["k_" + n], 1)
 
     def pa(t, a=None, b=None):
         return t[0:16, :] if a is None else t[0:16, a:b]
 
     v.wait_ge(S.lst, 32)
-    done(v.tensor_tensor(pa(T.l_x, L2, L3), pa(T.l_x, 0, L), pa(T.lns), ADD))
-    done(v.tensor_scalar(pa(T.l_x, L, L2), pa(T.l_x, 0, L), -1.0, None, ADD))
-    done(v.tensor_scalar(pa(T.l_e), pa(T.l_x, 0, L), float(O_H), None, ADD))
-    sync_v()
-    done(v.tensor_scalar(pa(T.l_x, L3, L4), pa(T.l_x, L2, L3), -1.0, None, ADD))
-    sync_v()
-    done(v.tensor_scalar(pa(T.l_v1), pa(T.l_x), B1, None, SHR))
-    done(v.tensor_scalar(pa(T.l_v2), pa(T.l_x), B2, None, SHR))
-    sync_v()
-    done(v.tensor_tensor(pa(T.l_d, 0, L2), pa(T.l_v1, L2, L4), pa(T.l_v1, 0, L2), SUB))
-    done(v.tensor_tensor(pa(T.l_d, L2, L4), pa(T.l_v2, L2, L4), pa(T.l_v2, 0, L2), SUB))
-    done(v.tensor_scalar(pa(T.l_pm), pa(T.l_v1, 0, L), PER - 1, None, AND))
-    done(v.tensor_scalar(pa(T.l_hi), pa(T.l_v2, 0, L), 3, None, SHR))
-    done(v.tensor_scalar(pa(T.l_q8), pa(T.l_v2, L2, L3), 8.0, None, MUL))
-    sync_v()
-    done(v.tensor_scalar(pa(T.l_u), pa(T.l_d), 1.0, float(NT), MIN, MUL))
-    done(v.tensor_scalar(pa(T.l_g, 0, L3), pa(T.l_d, 0, L3), 2.0, None, GE))
-    sync_v()
-    done(v.tensor_tensor(pa(T.l_c), pa(T.l_u, 0, L2), pa(T.l_u, L2, L4), ADD))
-    done(v.tensor_scalar(pa(T.l_pm5), pa(T.l_pm), float(NT), float(PH - 1 - ZERO), MUL, ADD))
-    done(v.tensor_scalar(pa(T.l_hi5), pa(T.l_hi), float(NT - 8), float(-8 - ZERO), MUL, ADD))
-    done(v.tensor_tensor(pa(T.l_f1), pa(T.l_q8), pa(T.l_v2, 0, L), ADD))
-    sync_v()
-    done(v.tensor_tensor(pa(T.l_o, 0, L), pa(T.l_e), pa(T.l_c, 0, L), SUB))
-    done(v.tensor_tensor(pa(T.l_o, L, L2), pa(T.l_x, L3, L4), pa(T.l_c, L, L2), ADD))
-    done(v.tensor_tensor(pa(T.l_fp, 0, L), pa(T.l_f1), pa(T.l_hi5), ADD))
-    done(v.tensor_tensor(pa(T.l_fp, L, L2), pa(T.l_v1, L2, L3), pa(T.l_pm5), ADD))
-    done(v.tensor_tensor(pa(T.l_g, L3, L4), pa(T.l_g, 0, L), pa(T.l_u, L2, L3), GT))
-    sync_v()
+    op("t", v.tensor_tensor(pa(T.l_x, L2, L3), pa(T.l_x, 0, L), pa(T.lns), ADD))
+    op("l1", v.tensor_scalar(pa(T.l_x, L, L2), pa(T.l_x, 0, L), -1.0, None, ADD))
+    need("t")
+    op("r", v.tensor_scalar(pa(T.l_x, L3, L4), pa(T.l_x, L2, L3), -1.0, None, ADD))
+    op("e", v.tensor_scalar(pa(T.l_e), pa(T.l_x, 0, L), float(O_H), None, ADD))
+    need("l1", "r")
+    op("v1", v.tensor_scalar(pa(T.l_v1), pa(T.l_x), B1, None, SHR))
+    op("v2", v.tensor_scalar(pa(T.l_v2), pa(T.l_x), B2, None, SHR))
+    need("v1")
+    op("d1", v.tensor_tensor(pa(T.l_d, 0, L2), pa(T.l_v1, L2, L4), pa(T.l_v1, 0, L2), SUB))
+    need("v2")
+    op("d2", v.tensor_tensor(pa(T.l_d, L2, L4), pa(T.l_v2, L2, L4), pa(T.l_v2, 0, L2), SUB))
+    op("pm", v.tensor_scalar(pa(T.l_pm), pa(T.l_v1, 0, L), PER - 1, None, AND))
+    need("d1", "d2")
+    op("u", v.tensor_scalar(pa(T.l_u), pa(T.l_d), 1.0, float(NT), MIN, MUL))
+    op("hi", v.tensor_scalar(pa(T.l_hi), pa(T.l_v2, 0, L), 3, None, SHR))
+    need("u")
+    op("c", v.tensor_tensor(pa(T.l_c), pa(T.l_u, 0, L2), pa(T.l_u, L2, L4), ADD))
+    op("g", v.tensor_scalar(pa(T.l_g, 0, L3), pa(T.l_d, 0, L3), 2.0, None, GE))
+    need("c", "e")
+    op("o0", v.tensor_tensor(pa(T.l_o, 0, L), pa(T.l_e), pa(T.l_c, 0, L), SUB))
+    op("o1", v.tensor_tensor(pa(T.l_o, L, L2), pa(T.l_x, L3, L4), pa(T.l_c, L, L2), ADD))
+    op("q8", v.tensor_scalar(pa(T.l_q8), pa(T.l_v2, L2, L3), 8.0, None, MUL))
+    need("o0", "o1")
     v.tensor_copy(pa(T.offsl), pa(T.l_o)).then_inc(S.o1, 1)
-    done(v.tensor_tensor(pa(T.l_m), pa(T.l_fp), pa(T.l_g, L2, L4), MUL))
-    sync_v()
-    done(v.tensor_tensor(pa(T.l_r), pa(T.l_m, 0, L), pa(T.l_m, L, L2), ADD))
 
     def quant_a(lo, hi, load, q):
         v.wait_ge(load, 16)
         v.quantize_mx(T.aq[:, lo:hi], T.ap_[:, lo:hi], T.as_[:, 4 * lo:4 * hi]).then_inc(q, 1)
 
-    def quant_x(lo, hi, load):
+    def quant_x(lo, hi, load, q):
         v.wait_ge(load, 16)
-        v.quantize_mx(T.xq[:, lo:hi], T.xp[:, lo:hi], T.xs[:, 4 * lo:4 * hi]).then_inc(S.qx, 1)
+        v.quantize_mx(T.xq[:, lo:hi], T.xp[:, lo:hi], T.xs[:, 4 * lo:4 * hi]).then_inc(q, 1)
 
-    quant_x(0, NT // 2, S.lx0)
+    quant_x(0, XH, S.lx0, S.qx0)
     quant_a(0, 128, S.la0, S.qa0)
-    quant_x(NT // 2, NT, S.lx1)
-    sync_v()
-    v.tensor_scalar(pa(T.offrl), pa(T.l_r), float(ZERO), None, ADD).then_inc(S.o2, 1)
+    quant_x(XH, NT, S.lx1, S.qx1)
 
-    v.memset(T.mk[:, K2:KALL], 1.0).then_inc(S.vm, 1)
-    v.memset(T.runs[:, ZERO:2 * NT:8], 0.0).then_inc(S.rs, 1)
+    need("hi", "q8")
+    op("hi5", v.tensor_scalar(pa(T.l_hi5), pa(T.l_hi), float(8 * AGAIN - 8), float(-8 - ZERO), MUL, ADD))
+    op("f1", v.tensor_tensor(pa(T.l_f1), pa(T.l_q8), pa(T.l_v2, 0, L), ADD))
+    need("pm")
+    op("pm5", v.tensor_scalar(pa(T.l_pm5), pa(T.l_pm), float(NT), float(PH - 1 - ZERO), MUL, ADD))
+    need("g")
+    op("gp", v.tensor_tensor(pa(T.l_g, L3, L4), pa(T.l_g, 0, L), pa(T.l_u, L2, L3), GT))
+    need("hi5", "f1")
+    op("f", v.tensor_tensor(pa(T.l_fp, 0, L), pa(T.l_f1), pa(T.l_hi5), ADD))
+    need("pm5")
+    op("p", v.tensor_tensor(pa(T.l_fp, L, L2), pa(T.l_v1, L2, L3), pa(T.l_pm5), ADD))
+    need("gp", "f", "p")
+    op("m", v.tensor_tensor(pa(T.l_m), pa(T.l_fp), pa(T.l_g, L2, L4), MUL))
     quant_a(128, 256, S.la1, S.qa1)
-    v.wait_ge(S.vm, 3)
-    v.memset(T.mk[:, K2:K2 + NT:W2], 0.0).then_inc(S.vm, 1)
-    v.memset(T.mk[:, K8:K8 + NT + PER:PER], 0.0).then_inc(S.vm, 1)
-    v.memset(T.mk[:, K16:KALL:N2], 0.0).then_inc(S.vm, 1)
+    need("m")
+    op("sum", v.tensor_tensor(pa(T.l_r), pa(T.l_m, 0, L), pa(T.l_m, L, L2), ADD))
+    need("sum")
+    v.tensor_scalar(pa(T.offrl), pa(T.l_r), float(ZERO), None, ADD).then_inc(S.o2, 1)
 
     sy.wait_ge(S.o1, 1)
     for k in range(8):
@@ -238,17 +247,27 @@ def rank_program(g, core, T, topo):
         sy.dma_start(T.pfs[16 * k:16 * k + 16, :], T.pf[:, :]).then_inc(S.lpl, 16)
         sy.dma_start(T.pgs[16 * k:16 * k + 16, :], T.pg[:, :]).then_inc(S.lpl, 16)
 
-    te.wait_ge(S.qx, 2)
-    for i in range(4):
-        if i < 3:
-            te.wait_ge((S.qa0, S.qa1, S.qa2)[i], 1)
-        te.matmul_mx(T.z[:, 512 * i:512 * i + NT], T.aq[:, 128 * i:128 * i + 128], T.ap_[:, 128 * i:128 * i + 128],
-                     T.xq[:, :], T.xp[:, :], True, True).then_inc(S["mm%d" % i], 1)
+    ZH = 2048
 
-    def relu(i):
-        s.wait_ge(S["mm%d" % i], 1)
-        s.activation(T.win[:, i * W + O_H:i * W + O_H + NT], T.z[:, 512 * i:512 * i + NT], RELU, scale=0.05).then_inc(
-            S["rl%d" % i], 1)
+    def product(out, n, i, c, sem):
+        te.matmul_mx(T.z[:, out:out + n], T.aq[:, 128 * i:128 * i + 128], T.ap_[:, 128 * i:128 * i + 128],
+                     T.xq[:, c:c + n], T.xp[:, c:c + n], True, True).then_inc(sem, 1)
+
+    te.wait_ge(S.qx0, 1)
+    te.wait_ge(S.qa0, 1)
+    product(ZH, XH, 0, 0, S.mmh)
+    te.wait_ge(S.qx1, 1)
+    product(0, XH, 0, XH, S.mm0)
+    te.wait_ge(S.qa1, 1)
+    product(512, NT, 1, 0, S.mm1)
+    te.wait_ge(S.qa2, 1)
+    product(1024, NT, 2, 0, S.mm2)
+    product(1536, NT, 3, 0, S.mm3)
+
+    def relu(i, frm, n, c, sem):
+        s.wait_ge(sem, 1)
+        h = i * W + O_H + c
+        s.activation(T.win[:, h:h + n], T.z[:, frm:frm + n], RELU, scale=0.05).then_inc(S["rl%d" % i], 1)
 
     def per(i):
         return 2 if i in BY_V else 3
@@ -267,34 +286,36 @@ def rank_program(g, core, T, topo):
     def runs(i, a):
         return T.runs[:, i * N1:WR].indirect(T.offr[:, a // 16:(a + HALF) // 16])
 
-    relu(0)
-    relu(1)
+    relu(0, ZH, XH, 0, S.mmh)
+    relu(0, 0, XH, XH, S.mm0)
+    relu(1, 512, NT, 0, S.mm1)
     s.wait_ge(S.rep, 128)
     gather_p(0)
-    relu(2)
-    relu(3)
+    relu(2, 1024, NT, 0, S.mm2)
+    relu(3, 1536, NT, 0, S.mm3)
     gather_s(0)
     for i in (1, 2, 3):
         gather_p(i)
         gather_s(i)
-    n_runs = 1 + (PER - 2) + (N2 - 1)
+    n_runs = 1 + (PER - 3) + 8
     s.wait_ge(S.rs, n_runs)
     s.wait_ge(S.repr_, 128)
-    for a, sem in ((fs, "grf%d"), (ns, "grn%d")):
-        for i in range(4):
-            if i not in BY_V:
-                s.activation(T["g%d" % i][:, 3 * a + 2:3 * (a + HALF):3], runs(i, a), COPY).then_inc(S[sem % i], 1)
+    for a, sem in ((fs, S.grf), (ns, S.grn)):
+        s.activation(T.g0[:, 3 * a + 2:3 * (a + HALF):3], runs(0, a), COPY).then_inc(sem, 1)
+
+    def pick(d, first, b, w, n, sem):
+        g.affine_select(d[:, first:first + n], T.win[:, b + w - 1:b + NT:w], [[0, n]], EQ, 0.0, 0, 0).then_inc(sem, 1)
 
     for i in range(4):
-        for sem, o, w, n, d, ds in (("p1_%d", O_P1, W1, N1, T.d1, S.d1s), ("p2_%d", O_P2, W2, N2, T.d2, S.d2s)):
-            g.wait_ge(S[sem % i], 1)
-            b = i * W + o
-            g.affine_select(d[:, i * n:(i + 1) * n], T.win[:, b + w - 1:b + NT:w], [[0, n]], EQ, 0.0, 0, 0).then_inc(
-                ds, 1)
+        g.wait_ge(S["p1_%d" % i], 1)
+        pick(T.runs, D1 + i * N1, i * W + O_P1, W1, N1, S.d1s)
+        g.wait_ge(S["p2_%d" % i], 1)
+        for o in (0, AGAIN):
+            pick(T.d2, o + i * N2, i * W + O_P2, W2, N2, S.d2s)
 
     def build_p(i):
         w = i * W
-        v.wait_ge(S["rl%d" % i], 1)
+        v.wait_ge(S["rl%d" % i], 1 if i else 2)
         for o, k, sem in ((O_P1, K1, "p1_%d"), (O_P2, K2, "p2_%d")):
             v.tensor_tensor_scan(T.win[:, w + o:w + o + NT], T.mk[:, k:k + NT], T.win[:, w + O_H:w + O_H + NT], 0.0,
                                  MUL, MAX).then_inc(S[sem % i], 1)
@@ -305,7 +326,7 @@ def rank_program(g, core, T, topo):
             v.tensor_tensor_scan(rev(T.win, w + o, w + o + NT), T.mk[:, k:k + NT],
                                  rev(T.win, w + O_H, w + O_H + NT), 0.0, MUL, MAX).then_inc(S["ss%d" % i], 1)
 
-    v.wait_ge(S.vm, 6)
+    v.wait_ge(S.vm, 5)
     build_p(0)
     quant_a(256, 512, S.la2, S.qa2)
     build_s(0)
@@ -313,57 +334,60 @@ def rank_program(g, core, T, topo):
         build_p(i)
         build_s(i)
     v.wait_ge(S.d1s, 4)
-    for m in range(PER - 2):
+    for m in range(PER - 3):
         k, o = K8 + PER - 1 - m, PH + m * NT
-        v.tensor_tensor_scan(T.runs[:, o:o + NT], T.mk[:, k:k + NT], T.d1[:, :], 0.0, MUL, MAX).then_inc(S.rs, 1)
-    v.wait_ge(S.d2s, 4)
-    for q in range(N2 - 1):
-        k, o = K16 + N2 - 1 - q, (q >> 3) * NT
-        v.tensor_tensor_scan(T.runs[:, o + (q & 7):o + NT:8], T.mk[:, k:k + 4 * N2], T.d2[:, :], 0.0,
-                             MUL, MAX).then_inc(S.rs, 1)
+        v.tensor_tensor_scan(T.runs[:, o:o + NT], T.mk[:, k:k + NT], T.runs[:, D1:WR], 0.0, MUL, MAX).then_inc(S.rs, 1)
+    v.wait_ge(S.d2s, 8)
+    v.wait_ge(S.zero, 1)
+    for q in range(8):
+        k, n = K16 + N2 - 1 - q, D2 if q < 7 else ND
+        v.tensor_tensor_scan(T.runs[:, q:8 * n:8], T.mk[:, k:k + n], T.d2[:, 0:n], 0.0, MUL, MAX).then_inc(S.rs, 1)
 
-    def scan(i, a, sem):
+    def scan(i, a):
         k = per(i)
         m = (PAIR if k == 2 else TRI)
         v.tensor_tensor_scan(T["m%d" % i][:, k * a:k * (a + HALF)], T.mg[:, m:m + k * HALF],
-                             T["g%d" % i][:, k * a:k * (a + HALF)], 0.0, MUL, MAX).then_inc(S[sem % i], 1)
+                             T["g%d" % i][:, k * a:k * (a + HALF)], 0.0, MUL, MAX).then_inc(
+            S[("mef%d" if a == fs else "men%d") % i], 1)
 
-    def merged(i, a, sem, out):
+    def merged(i, a):
         k = per(i)
         M = T["m%d" % i][:, k * a + k - 1:k * (a + HALF):k]
         dst = T.tile[:, 4 * a + i:4 * (a + HALF):4]
-        v.wait_ge(S[sem % i], 1)
+        out = S.tlf if a == fs else S.tln
+        v.wait_ge(S[("mef%d" if a == fs else "men%d") % i], 1)
         if k == 2:
             v.tensor_tensor(dst, runs(i, a), M, MAX).then_inc(out, 1)
         else:
             v.tensor_copy(dst, M).then_inc(out, 1)
 
     v.wait_ge(S.gm, 2)
-    v.wait_ge(S.ge2, 2)
-    scan(2, fs, "mef%d")
-    scan(2, ns, "men%d")
+    for i in (1, 2):
+        v.wait_ge(S["ge%d" % i], 2)
+        scan(i, fs)
+        scan(i, ns)
     v.wait_ge(S.rs, n_runs)
     v.wait_ge(S.repr_, 128)
-    merged(2, fs, "mef%d", S.tlf)
-    merged(2, ns, "men%d", S.tln)
+    merged(1, fs)
+    merged(2, fs)
+    merged(1, ns)
     v.wait_ge(S.ge3, 2)
-    scan(3, fs, "mef%d")
-    scan(3, ns, "men%d")
-    merged(3, fs, "mef%d", S.tlf)
-    for a, gr, me, tl in ((fs, "grf%d", "mef%d", S.tlf), (ns, "grn%d", "men%d", S.tln)):
-        for i in (0, 1):
-            v.wait_ge(S["ge%d" % i], 2)
-            v.wait_ge(S[gr % i], 1)
-            scan(i, a, me)
-        merged(0, a, me, tl)
-        if a == ns:
-            merged(3, ns, me, tl)
-        merged(1, a, me, tl)
-        v.wait_ge(tl, 4)
-        if a == fs:
-            v.quantize_mx(T.fq[:, :], T.fp[:, :], T.tile[:, 4 * fs:4 * (fs + HALF)]).then_inc(S.qf, 1)
-        else:
-            v.quantize_mx(T.nq[:, :], T.np_[:, :], T.tile[:, 4 * ns:4 * (ns + HALF)]).then_inc(S.qn, 1)
+    scan(3, fs)
+    v.wait_ge(S.ge0, 2)
+    v.wait_ge(S.grf, 1)
+    scan(0, fs)
+    merged(3, fs)
+    merged(0, fs)
+    v.wait_ge(S.tlf, 4)
+    v.quantize_mx(T.fq[:, :], T.fp[:, :], T.tile[:, 4 * fs:4 * (fs + HALF)]).then_inc(S.qf, 1)
+    scan(3, ns)
+    merged(2, ns)
+    v.wait_ge(S.grn, 1)
+    scan(0, ns)
+    merged(3, ns)
+    merged(0, ns)
+    v.wait_ge(S.tln, 4)
+    v.quantize_mx(T.nq[:, :], T.np_[:, :], T.tile[:, 4 * ns:4 * (ns + HALF)]).then_inc(S.qn, 1)
 
     n_loc = [0]
 
@@ -405,19 +429,21 @@ def rank_program(g, core, T, topo):
     me = near.index(rank) * CAPP
     sy.wait_ge(S.qn, 1)
     sy.dma_start(T.rnq[:, me:me + CAPP].bitcast(dt.uint8), T.nq[:, me:me + CAPP].bitcast(dt.uint8)).then_inc(S.own, 16)
-    sy.dma_start(T.rnp[:, me:me + CAPP], T.np_[:, me:me + CAPP]).then_inc(S.own, 16)
+    s.wait_ge(S.qn, 1)
+    s.dma_start(T.rnp[:, me:me + CAPP], T.np_[:, me:me + CAPP]).then_inc(S.own, 16)
 
     v.wait_ge(S.luv, 32)
     v.quantize_mx(T.vq[:, :], T.vp[:, :], T.vs[:, :]).then_inc(S.quv, 1)
     v.quantize_mx(T.uq[:, :], T.up[:, :], T.us[:, :]).then_inc(S.quv, 1)
     v.wait_ge(S.lpl, 256)
-    done(v.tensor_scalar(T.pgt[:, :], T.pgs[:, :], 0.0, float(ZCOL + 1), LT, MUL))
+    op("pgt", v.tensor_scalar(T.pgt[:, :], T.pgs[:, :], 0.0, float(ZCOL + 1), LT, MUL))
     v.tensor_copy(T.pfo[:, :], T.pfs[:, :]).then_inc(S.pl, 1)
-    sync_v()
-    done(v.tensor_tensor(T.pgn[:, :], T.pgs[:, :], T.pgt[:, :], ADD))
-    sync_v()
+    need("pgt")
+    op("pgn", v.tensor_tensor(T.pgn[:, :], T.pgs[:, :], T.pgt[:, :], ADD))
+    v.memset(T.zu[:, ZCOL:ZCOL + 16], 0.0).then_inc(S.zero, 1)
+    need("pgn")
     v.tensor_copy(T.pgo[:, :], T.pgn[:, :]).then_inc(S.pl, 1)
-    v.wait_ge(S.zero, 1)
+    v.wait_ge(S.zero, 2)
 
     te.wait_ge(S.quv, 2)
     for k, (arr, n, cq, cp, first, sv, su) in enumerate((

from concourse.bass import DstId, RemoteDMATransfer
from concourse.mybir import dt, AluOpType, ActivationFunctionType

N, CAPP, NT, P = 8, 48, 512, 256
SL = N * CAPP
LC = SL // 16
HALF = SL // 2
B1, B2 = 2, 5
W1, W2 = 1 << B1, 1 << B2
N1, N2 = NT // W1, NT // W2
PER = W2 // W1
O_S2, O_S1, O_H, O_P1, O_P2 = 0, NT, 2 * NT, 3 * NT, 4 * NT
W = 5 * NT
ND = 4 * N2
AGAIN = ND + 8
D2 = AGAIN + ND
PH = 8 * D2
D1 = PH + (PER - 3) * NT
WR = D1 + NT
ZERO = 8 * AGAIN + 7
K1, K2, K8, K16 = 0, NT, 2 * NT, 3 * NT + PER
KALL = K16 + D2 + N2
TRI, PAIR = 0, 3 * HALF
KG = 5 * HALF
ZCOL = SL
BY_V = (1, 2, 3)

SCRATCH = {
    "xs": ("sbuf", [128, 4 * NT], "bfloat16"),
    "as_": ("sbuf", [128, 2048], "bfloat16"),
    "us": ("sbuf", [128, 512], "bfloat16"),
    "vs": ("sbuf", [128, 512], "bfloat16"),
    "xq": ("sbuf", [128, NT], "float8_e4m3fn_x4"),
    "xp": ("sbuf", [128, NT], "uint8"),
    "aq": ("sbuf", [128, 512], "float8_e4m3fn_x4"),
    "ap_": ("sbuf", [128, 512], "uint8"),
    "uq": ("sbuf", [128, 128], "float8_e4m3fn_x4"),
    "up": ("sbuf", [128, 128], "uint8"),
    "vq": ("sbuf", [128, 128], "float8_e4m3fn_x4"),
    "vp": ("sbuf", [128, 128], "uint8"),
    "z": ("psum", [128, 4096], "float32"),
    "win": ("sbuf", [128, 4 * W], "bfloat16"),
    "runs": ("sbuf", [128, WR], "bfloat16"),
    "d2": ("sbuf", [128, D2], "bfloat16"),
    "mk": ("sbuf", [128, KALL], "bfloat16"),
    "mg": ("sbuf", [128, KG], "bfloat16"),
    "tile": ("sbuf", [128, 4 * SL], "bfloat16"),
    "fq": ("sbuf", [128, HALF], "float8_e4m3fn_x4"),
    "fp": ("sbuf", [128, HALF], "uint8"),
    "nq": ("sbuf", [128, HALF], "float8_e4m3fn_x4"),
    "np_": ("sbuf", [128, HALF], "uint8"),
    "rfq": ("sbuf", [128, HALF], "float8_e4m3fn_x4"),
    "rfp": ("sbuf", [128, HALF], "uint8"),
    "rnq": ("sbuf", [128, HALF], "float8_e4m3fn_x4"),
    "rnp": ("sbuf", [128, HALF], "uint8"),
    "zv": ("sbuf", [128, SL], "float32"),
    "zu": ("sbuf", [128, SL + 16], "float32"),
    "gy": ("sbuf", [128, P], "float32"),
    "ys": ("sbuf", [128, P], "float32"),
    "offs": ("sbuf", [128, 2 * LC], "uint16"),
    "offr": ("sbuf", [128, LC], "uint16"),
    "offsl": ("sbuf", [128, 2 * LC], "uint16"),
    "offrl": ("sbuf", [128, LC], "uint16"),
    "l_x": ("sbuf", [128, 4 * LC], "int32"),
    "lns": ("sbuf", [128, LC], "int32"),
    "l_e": ("sbuf", [128, LC], "int32"),
    "l_v1": ("sbuf", [128, 4 * LC], "int32"),
    "l_v2": ("sbuf", [128, 4 * LC], "int32"),
    "l_d": ("sbuf", [128, 4 * LC], "int32"),
    "l_u": ("sbuf", [128, 4 * LC], "int32"),
    "l_c": ("sbuf", [128, 2 * LC], "int32"),
    "l_g": ("sbuf", [128, 4 * LC], "int32"),
    "l_o": ("sbuf", [128, 2 * LC], "int32"),
    "l_pm": ("sbuf", [128, LC], "int32"),
    "l_hi": ("sbuf", [128, LC], "int32"),
    "l_q8": ("sbuf", [128, LC], "int32"),
    "l_pm5": ("sbuf", [128, LC], "int32"),
    "l_hi5": ("sbuf", [128, LC], "int32"),
    "l_f1": ("sbuf", [128, LC], "int32"),
    "l_fp": ("sbuf", [128, 2 * LC], "int32"),
    "l_m": ("sbuf", [128, 2 * LC], "int32"),
    "l_r": ("sbuf", [128, LC], "int32"),
    "pfs": ("sbuf", [128, P // 16], "int32"),
    "pgs": ("sbuf", [128, P // 16], "int32"),
    "pgt": ("sbuf", [128, P // 16], "int32"),
    "pgn": ("sbuf", [128, P // 16], "int32"),
    "pfo": ("sbuf", [128, P // 16], "uint16"),
    "pgo": ("sbuf", [128, P // 16], "uint16"),
}
for _i in range(4):
    _k = 2 if _i in BY_V else 3
    SCRATCH["g%d" % _i] = ("sbuf", [128, _k * SL], "bfloat16")
    SCRATCH["m%d" % _i] = ("sbuf", [128, _k * SL], "bfloat16")

STEPS = ["t", "l1", "e", "r", "v1", "v2", "d1", "d2", "pm", "u", "hi", "c", "g", "o0", "o1", "q8", "pm5", "hi5", "f1",
         "gp", "f", "p", "m", "sum", "pgt", "pgn"]

SEMAPHORES = (["lst", "lx0", "lx1", "la0", "la1", "la2", "luv", "lpl", "rep", "repr_", "o1", "o2", "vm",
               "qx0", "qx1", "qa0", "qa1", "qa2", "quv", "gi", "gm", "d1s", "d2s", "rs", "mmh",
               "qf", "qn", "zero", "pl", "own", "arrf", "arrn", "loc", "mfv", "mfu", "mnv", "mnu", "zvs", "zus",
               "gy0", "gy1", "y0", "y1", "yo", "tlf", "tln", "grf", "grn"]
              + ["k_%s" % _n for _n in STEPS]
              + ["%s%d" % (_n, _i) for _i in range(4)
                 for _n in ("mm", "rl", "p1_", "p2_", "ss", "ge", "mef", "men")])

ADD, SUB, MUL, MAX, MIN = AluOpType.add, AluOpType.subtract, AluOpType.mult, AluOpType.max, AluOpType.min
GE, GT, LT, NEQ, EQ = AluOpType.is_ge, AluOpType.is_gt, AluOpType.is_lt, AluOpType.not_equal, AluOpType.is_equal
SHR, AND = AluOpType.arith_shift_right, AluOpType.bitwise_and
RELU, COPY = ActivationFunctionType.Relu, ActivationFunctionType.Copy


def rev(t, lo, hi):
    return t[:, hi - 1:(lo - 1 if lo > 0 else None):-1]


def engine_plan(core, dests, topo):
    off = [d for d in dests if topo.chip(d) != topo.chip(core)]
    pool = topo.engines(core, off[0])
    per = 1
    while 2 * per * len(off) <= len(pool):
        per *= 2
    masks = {}
    for k, d in enumerate(off):
        masks[d] = pool[k * per:(k + 1) * per]
    for d in dests:
        if d not in masks:
            masks[d] = [e for e in topo.engines(core, d) if e not in pool][:2]
    return masks


def rank_program(g, core, T, topo):
    rank = T.rank_of(core)
    if rank is None:
        return
    cores = T.cores
    S = T.sem
    v, s, te, sy = g.vector, g.scalar, g.tensor, g.sync

    def group(c, far):
        a = topo.chip(c)
        return [q for q in range(N)
                if (topo.chip(cores[q]) != a and not topo.mates(topo.chip(cores[q]), a)) == far]

    far, near = group(core, True), group(core, False)
    fs, ns = far[0] * CAPP, near[0] * CAPP
    L, L2, L3, L4 = LC, 2 * LC, 3 * LC, 4 * LC
    XH = NT // 2

    s.dma_start(T.l_x[0:16, 0:L], T.lo[:, :]).then_inc(S.lst, 16)
    sy.dma_start(T.lns[0:16, :], T.ln[:, :]).then_inc(S.lst, 16)
    sy.dma_start(T.xs[:, 0:4 * XH], T.x[:, 0:4 * XH]).then_inc(S.lx0, 16)
    s.dma_start(T.as_[:, 0:512], T.a[:, 0:512]).then_inc(S.la0, 16)
    sy.dma_start(T.xs[:, 4 * XH:4 * NT], T.x[:, 4 * XH:4 * NT]).then_inc(S.lx1, 16)
    sy.dma_start(T.as_[:, 512:1024], T.a[:, 512:1024]).then_inc(S.la1, 16)
    sy.dma_start(T.as_[:, 1024:2048], T.a[:, 1024:2048]).then_inc(S.la2, 16)

    g.iota(T.mg[:, :], [[0, KG]], 1, 0, allow_small_or_imprecise_dtypes=True).then_inc(S.gi, 1)
    g.wait_ge(S.gi, 1)
    for o, k in ((TRI, 3), (PAIR, 2)):
        m = T.mg[:, o:o + k * HALF]
        g.affine_select(m, m, [[0, HALF], [1, k]], NEQ, 0.0, 0, 0).then_inc(S.gm, 1)

    v.memset(T.mk[:, :], 1.0).then_inc(S.vm, 1)
    v.memset(T.runs[:, 8 * ND + 7:PH:8], 0.0).then_inc(S.rs, 1)
    v.memset(T.d2[:, ND:AGAIN], 0.0).then_inc(S.zero, 1)
    v.wait_ge(S.vm, 1)
    for b, e, w in ((K1, K2, W1), (K2, K8, W2), (K8, K16, PER), (K16, KALL, N2)):
        v.memset(T.mk[:, b:e:w], 0.0).then_inc(S.vm, 1)

    def op(name, ins):
        ins.then_inc(S["k_" + name], 1)

    def need(*names):
        for n in names:
            v.wait_ge(S["k_" + n], 1)

    def pa(t, a=None, b=None):
        return t[0:16, :] if a is None else t[0:16, a:b]

    v.wait_ge(S.lst, 32)
    op("t", v.tensor_tensor(pa(T.l_x, L2, L3), pa(T.l_x, 0, L), pa(T.lns), ADD))
    op("l1", v.tensor_scalar(pa(T.l_x, L, L2), pa(T.l_x, 0, L), -1.0, None, ADD))
    need("t")
    op("r", v.tensor_scalar(pa(T.l_x, L3, L4), pa(T.l_x, L2, L3), -1.0, None, ADD))
    op("e", v.tensor_scalar(pa(T.l_e), pa(T.l_x, 0, L), float(O_H), None, ADD))
    need("l1", "r")
    op("v1", v.tensor_scalar(pa(T.l_v1), pa(T.l_x), B1, None, SHR))
    op("v2", v.tensor_scalar(pa(T.l_v2), pa(T.l_x), B2, None, SHR))
    need("v1")
    op("d1", v.tensor_tensor(pa(T.l_d, 0, L2), pa(T.l_v1, L2, L4), pa(T.l_v1, 0, L2), SUB))
    need("v2")
    op("d2", v.tensor_tensor(pa(T.l_d, L2, L4), pa(T.l_v2, L2, L4), pa(T.l_v2, 0, L2), SUB))
    op("pm", v.tensor_scalar(pa(T.l_pm), pa(T.l_v1, 0, L), PER - 1, None, AND))
    need("d1", "d2")
    op("u", v.tensor_scalar(pa(T.l_u), pa(T.l_d), 1.0, float(NT), MIN, MUL))
    op("hi", v.tensor_scalar(pa(T.l_hi), pa(T.l_v2, 0, L), 3, None, SHR))
    need("u")
    op("c", v.tensor_tensor(pa(T.l_c), pa(T.l_u, 0, L2), pa(T.l_u, L2, L4), ADD))
    op("g", v.tensor_scalar(pa(T.l_g, 0, L3), pa(T.l_d, 0, L3), 2.0, None, GE))
    need("c", "e")
    op("o0", v.tensor_tensor(pa(T.l_o, 0, L), pa(T.l_e), pa(T.l_c, 0, L), SUB))
    op("o1", v.tensor_tensor(pa(T.l_o, L, L2), pa(T.l_x, L3, L4), pa(T.l_c, L, L2), ADD))
    op("q8", v.tensor_scalar(pa(T.l_q8), pa(T.l_v2, L2, L3), 8.0, None, MUL))
    need("o0", "o1")
    v.tensor_copy(pa(T.offsl), pa(T.l_o)).then_inc(S.o1, 1)

    def quant_a(lo, hi, load, q):
        v.wait_ge(load, 16)
        v.quantize_mx(T.aq[:, lo:hi], T.ap_[:, lo:hi], T.as_[:, 4 * lo:4 * hi]).then_inc(q, 1)

    def quant_x(lo, hi, load, q):
        v.wait_ge(load, 16)
        v.quantize_mx(T.xq[:, lo:hi], T.xp[:, lo:hi], T.xs[:, 4 * lo:4 * hi]).then_inc(q, 1)

    quant_x(0, XH, S.lx0, S.qx0)
    quant_a(0, 128, S.la0, S.qa0)
    quant_x(XH, NT, S.lx1, S.qx1)

    need("hi", "q8")
    op("hi5", v.tensor_scalar(pa(T.l_hi5), pa(T.l_hi), float(8 * AGAIN - 8), float(-8 - ZERO), MUL, ADD))
    op("f1", v.tensor_tensor(pa(T.l_f1), pa(T.l_q8), pa(T.l_v2, 0, L), ADD))
    need("pm")
    op("pm5", v.tensor_scalar(pa(T.l_pm5), pa(T.l_pm), float(NT), float(PH - 1 - ZERO), MUL, ADD))
    need("g")
    op("gp", v.tensor_tensor(pa(T.l_g, L3, L4), pa(T.l_g, 0, L), pa(T.l_u, L2, L3), GT))
    need("hi5", "f1")
    op("f", v.tensor_tensor(pa(T.l_fp, 0, L), pa(T.l_f1), pa(T.l_hi5), ADD))
    need("pm5")
    op("p", v.tensor_tensor(pa(T.l_fp, L, L2), pa(T.l_v1, L2, L3), pa(T.l_pm5), ADD))
    need("gp", "f", "p")
    op("m", v.tensor_tensor(pa(T.l_m), pa(T.l_fp), pa(T.l_g, L2, L4), MUL))
    quant_a(128, 256, S.la1, S.qa1)
    need("m")
    op("sum", v.tensor_tensor(pa(T.l_r), pa(T.l_m, 0, L), pa(T.l_m, L, L2), ADD))
    need("sum")
    v.tensor_scalar(pa(T.offrl), pa(T.l_r), float(ZERO), None, ADD).then_inc(S.o2, 1)

    sy.wait_ge(S.o1, 1)
    for k in range(8):
        sy.dma_start(T.offs[16 * k:16 * k + 16, :], pa(T.offsl)).then_inc(S.rep, 16)
    sy.wait_ge(S.o2, 1)
    for k in range(8):
        sy.dma_start(T.offr[16 * k:16 * k + 16, :], pa(T.offrl)).then_inc(S.repr_, 16)
    sy.dma_start(T.vs[:, :], T.v[:, :]).then_inc(S.luv, 16)
    sy.dma_start(T.us[:, :], T.u[:, :]).then_inc(S.luv, 16)
    for k in range(8):
        sy.dma_start(T.pfs[16 * k:16 * k + 16, :], T.pf[:, :]).then_inc(S.lpl, 16)
        sy.dma_start(T.pgs[16 * k:16 * k + 16, :], T.pg[:, :]).then_inc(S.lpl, 16)

    ZH = 2048

    def product(out, n, i, c, sem):
        te.matmul_mx(T.z[:, out:out + n], T.aq[:, 128 * i:128 * i + 128], T.ap_[:, 128 * i:128 * i + 128],
                     T.xq[:, c:c + n], T.xp[:, c:c + n], True, True).then_inc(sem, 1)

    te.wait_ge(S.qx0, 1)
    te.wait_ge(S.qa0, 1)
    product(ZH, XH, 0, 0, S.mmh)
    te.wait_ge(S.qx1, 1)
    product(0, XH, 0, XH, S.mm0)
    te.wait_ge(S.qa1, 1)
    product(512, NT, 1, 0, S.mm1)
    te.wait_ge(S.qa2, 1)
    product(1024, NT, 2, 0, S.mm2)
    product(1536, NT, 3, 0, S.mm3)

    def relu(i, frm, n, c, sem):
        s.wait_ge(sem, 1)
        h = i * W + O_H + c
        s.activation(T.win[:, h:h + n], T.z[:, frm:frm + n], RELU, scale=0.05).then_inc(S["rl%d" % i], 1)

    def per(i):
        return 2 if i in BY_V else 3

    def gather_p(i):
        s.wait_ge(S["p1_%d" % i], 1)
        s.wait_ge(S["p2_%d" % i], 1)
        s.activation(T["g%d" % i][:, 1::per(i)], T.win[:, i * W + O_H:i * W + W].indirect(T.offs[:, L:L2]),
                     COPY).then_inc(S["ge%d" % i], 1)

    def gather_s(i):
        s.wait_ge(S["ss%d" % i], 2)
        s.activation(T["g%d" % i][:, 0::per(i)], T.win[:, i * W:i * W + O_P1].indirect(T.offs[:, 0:L]),
                     COPY).then_inc(S["ge%d" % i], 1)

    def runs(i, a):
        return T.runs[:, i * N1:WR].indirect(T.offr[:, a // 16:(a + HALF) // 16])

    relu(0, ZH, XH, 0, S.mmh)
    relu(0, 0, XH, XH, S.mm0)
    relu(1, 512, NT, 0, S.mm1)
    s.wait_ge(S.rep, 128)
    gather_p(0)
    relu(2, 1024, NT, 0, S.mm2)
    relu(3, 1536, NT, 0, S.mm3)
    gather_s(0)
    for i in (1, 2, 3):
        gather_p(i)
        gather_s(i)
    n_runs = 1 + (PER - 3) + 8
    s.wait_ge(S.rs, n_runs)
    s.wait_ge(S.repr_, 128)
    for a, sem in ((fs, S.grf), (ns, S.grn)):
        s.activation(T.g0[:, 3 * a + 2:3 * (a + HALF):3], runs(0, a), COPY).then_inc(sem, 1)

    def pick(d, first, b, w, n, sem):
        g.affine_select(d[:, first:first + n], T.win[:, b + w - 1:b + NT:w], [[0, n]], EQ, 0.0, 0, 0).then_inc(sem, 1)

    for i in range(4):
        g.wait_ge(S["p1_%d" % i], 1)
        pick(T.runs, D1 + i * N1, i * W + O_P1, W1, N1, S.d1s)
        g.wait_ge(S["p2_%d" % i], 1)
        for o in (0, AGAIN):
            pick(T.d2, o + i * N2, i * W + O_P2, W2, N2, S.d2s)

    def build_p(i):
        w = i * W
        v.wait_ge(S["rl%d" % i], 1 if i else 2)
        for o, k, sem in ((O_P1, K1, "p1_%d"), (O_P2, K2, "p2_%d")):
            v.tensor_tensor_scan(T.win[:, w + o:w + o + NT], T.mk[:, k:k + NT], T.win[:, w + O_H:w + O_H + NT], 0.0,
                                 MUL, MAX).then_inc(S[sem % i], 1)

    def build_s(i):
        w = i * W
        for o, k in ((O_S1, K1), (O_S2, K2)):
            v.tensor_tensor_scan(rev(T.win, w + o, w + o + NT), T.mk[:, k:k + NT],
                                 rev(T.win, w + O_H, w + O_H + NT), 0.0, MUL, MAX).then_inc(S["ss%d" % i], 1)

    v.wait_ge(S.vm, 5)
    build_p(0)
    quant_a(256, 512, S.la2, S.qa2)
    build_s(0)
    for i in (1, 2, 3):
        build_p(i)
        build_s(i)
    v.wait_ge(S.d1s, 4)
    for m in range(PER - 3):
        k, o = K8 + PER - 1 - m, PH + m * NT
        v.tensor_tensor_scan(T.runs[:, o:o + NT], T.mk[:, k:k + NT], T.runs[:, D1:WR], 0.0, MUL, MAX).then_inc(S.rs, 1)
    v.wait_ge(S.d2s, 8)
    v.wait_ge(S.zero, 1)
    for q in range(8):
        k, n = K16 + N2 - 1 - q, D2 if q < 7 else ND
        v.tensor_tensor_scan(T.runs[:, q:8 * n:8], T.mk[:, k:k + n], T.d2[:, 0:n], 0.0, MUL, MAX).then_inc(S.rs, 1)

    def scan(i, a):
        k = per(i)
        m = (PAIR if k == 2 else TRI)
        v.tensor_tensor_scan(T["m%d" % i][:, k * a:k * (a + HALF)], T.mg[:, m:m + k * HALF],
                             T["g%d" % i][:, k * a:k * (a + HALF)], 0.0, MUL, MAX).then_inc(
            S[("mef%d" if a == fs else "men%d") % i], 1)

    def merged(i, a):
        k = per(i)
        M = T["m%d" % i][:, k * a + k - 1:k * (a + HALF):k]
        dst = T.tile[:, 4 * a + i:4 * (a + HALF):4]
        out = S.tlf if a == fs else S.tln
        v.wait_ge(S[("mef%d" if a == fs else "men%d") % i], 1)
        if k == 2:
            v.tensor_tensor(dst, runs(i, a), M, MAX).then_inc(out, 1)
        else:
            v.tensor_copy(dst, M).then_inc(out, 1)

    v.wait_ge(S.gm, 2)
    for i in (1, 2):
        v.wait_ge(S["ge%d" % i], 2)
        scan(i, fs)
        scan(i, ns)
    v.wait_ge(S.rs, n_runs)
    v.wait_ge(S.repr_, 128)
    merged(1, fs)
    merged(2, fs)
    merged(1, ns)
    v.wait_ge(S.ge3, 2)
    scan(3, fs)
    v.wait_ge(S.ge0, 2)
    v.wait_ge(S.grf, 1)
    scan(0, fs)
    merged(3, fs)
    merged(0, fs)
    v.wait_ge(S.tlf, 4)
    v.quantize_mx(T.fq[:, :], T.fp[:, :], T.tile[:, 4 * fs:4 * (fs + HALF)]).then_inc(S.qf, 1)
    scan(3, ns)
    merged(2, ns)
    v.wait_ge(S.grn, 1)
    scan(0, ns)
    merged(3, ns)
    merged(0, ns)
    v.wait_ge(S.tln, 4)
    v.quantize_mx(T.nq[:, :], T.np_[:, :], T.tile[:, 4 * ns:4 * (ns + HALF)]).then_inc(S.qn, 1)

    n_loc = [0]

    def send(isfar, mine, src_q, src_p, dst_q, dst_p, arr):
        dests = [q for q in mine if q != rank]
        masks = engine_plan(core, [cores[q] for q in dests], topo)
        for codes in (True, False):
            tr = []
            for q in dests:
                a = mine.index(q) * CAPP
                b = group(cores[q], isfar).index(rank) * CAPP
                rid, pid, _se = topo.addr(cores[q])
                m = 0
                for e in masks[cores[q]]:
                    m |= 1 << e
                    n_loc[0] += 1
                if codes:
                    src, dst = src_q[:, a:a + CAPP].bitcast(dt.uint8), dst_q[:, b:b + CAPP].bitcast(dt.uint8)
                else:
                    src, dst = src_p[:, a:a + CAPP], dst_p[:, b:b + CAPP]
                tr.append(RemoteDMATransfer(dst_ids=[DstId(rid=rid, pnc=pid)], dma_engine_mask=m, remote_sem=arr,
                                            src=src, dst=dst))
            g.remote_dma_fused(tr, local_sem=S.loc)

    def arrivals(isfar, mine):
        n = 0
        for q in mine:
            if q != rank:
                peers = [cores[p] for p in group(cores[q], isfar) if p != q]
                n += 2 * len(engine_plan(cores[q], peers, topo)[core])
        return n

    g.wait_ge(S.qf, 1)
    send(True, far, T.fq, T.fp, T.rfq, T.rfp, S.arrf)
    g.wait_ge(S.qn, 1)
    send(False, near, T.nq, T.np_, T.rnq, T.rnp, S.arrn)
    g.wait_ge(S.loc, n_loc[0])

    me = near.index(rank) * CAPP
    sy.wait_ge(S.qn, 1)
    sy.dma_start(T.rnq[:, me:me + CAPP].bitcast(dt.uint8), T.nq[:, me:me + CAPP].bitcast(dt.uint8)).then_inc(S.own, 16)
    s.wait_ge(S.qn, 1)
    s.dma_start(T.rnp[:, me:me + CAPP], T.np_[:, me:me + CAPP]).then_inc(S.own, 16)

    v.wait_ge(S.luv, 32)
    v.quantize_mx(T.vq[:, :], T.vp[:, :], T.vs[:, :]).then_inc(S.quv, 1)
    v.quantize_mx(T.uq[:, :], T.up[:, :], T.us[:, :]).then_inc(S.quv, 1)
    v.wait_ge(S.lpl, 256)
    op("pgt", v.tensor_scalar(T.pgt[:, :], T.pgs[:, :], 0.0, float(ZCOL + 1), LT, MUL))
    v.tensor_copy(T.pfo[:, :], T.pfs[:, :]).then_inc(S.pl, 1)
    need("pgt")
    op("pgn", v.tensor_tensor(T.pgn[:, :], T.pgs[:, :], T.pgt[:, :], ADD))
    v.memset(T.zu[:, ZCOL:ZCOL + 16], 0.0).then_inc(S.zero, 1)
    need("pgn")
    v.tensor_copy(T.pgo[:, :], T.pgn[:, :]).then_inc(S.pl, 1)
    v.wait_ge(S.zero, 2)

    te.wait_ge(S.quv, 2)
    for k, (arr, n, cq, cp, first, sv, su) in enumerate((
            (S.arrf, arrivals(True, far), T.rfq, T.rfp, fs, S.mfv, S.mfu),
            (S.arrn, arrivals(False, near), T.rnq, T.rnp, ns, S.mnv, S.mnu))):
        bv, bu = 2048 + 1024 * k, 2560 + 1024 * k
        te.wait_ge(arr, n)
        if k:
            te.wait_ge(S.own, 32)
        te.matmul_mx(T.z[:, bv:bv + HALF], T.vq[:, :], T.vp[:, :], cq[:, :], cp[:, :], True, True).then_inc(sv, 1)
        te.matmul_mx(T.z[:, bu:bu + HALF], T.uq[:, :], T.up[:, :], cq[:, :], cp[:, :], True, True).then_inc(su, 1)
        s.wait_ge(sv, 1)
        s.activation(T.zv[:, first:first + HALF], T.z[:, bv:bv + HALF], COPY).then_inc(S.zvs, 1)
        v.wait_ge(su, 1)
        v.tensor_copy(T.zu[:, first:first + HALF], T.z[:, bu:bu + HALF]).then_inc(S.zus, 1)

    h, hc = P // 2, P // 32
    s.wait_ge(S.pl, 2)
    s.wait_ge(S.zvs, 2)
    v.wait_ge(S.pl, 2)
    v.wait_ge(S.zus, 2)
    for k in range(2):
        gy, yy = (S.gy0, S.gy1)[k], (S.y0, S.y1)[k]
        s.activation(T.gy[:, k * h:k * h + h], T.zv[:, :].indirect(T.pfo[:, k * hc:k * hc + hc]), COPY).then_inc(gy, 1)
        v.wait_ge(gy, 1)
        v.tensor_tensor(T.ys[:, k * h:k * h + h], T.zu[:, :].indirect(T.pgo[:, k * hc:k * hc + hc]),
                        T.gy[:, k * h:k * h + h], ADD).then_inc(yy, 1)
        sy.wait_ge(yy, 1)
        sy.dma_start(T.y[:, k * h:k * h + h], T.ys[:, k * h:k * h + h]).then_inc(S.yo, 16)
    sy.wait_ge(S.yo, 32)
